import numpy as np, ml_dtypes
CORES = [83,85,87,115,117,119]
N = 6
import mx_ref
BF = ml_dtypes.bfloat16
def cols(t, e):
    v = np.concatenate([t.reshape(128, -1, 4), np.zeros((128, 1, 4), BF)], axis=1)
    return np.ascontiguousarray(v[:, e]).reshape(128, -1)
def cut(t, i, w=512):
    return t[:, w * i:w * i + w]
def pick(q, e):
    c = np.concatenate([q[0].reshape(128, -1, 4), np.zeros((128, 1, 4), np.uint8)], axis=1); s = np.concatenate([q[1], np.ones((16, 1), np.uint8)], axis=1)
    return (np.ascontiguousarray(c[:, e].reshape(128, -1)), np.ascontiguousarray(s[:, e]))
def join(*qs):
    return (np.concatenate([q[0] for q in qs], axis=1), np.concatenate([q[1] for q in qs], axis=1))
def put(q, e, v):
    c, s = q[0].reshape(128, -1, 4).copy(), q[1].copy(); c[:, e] = v[0].reshape(128, -1, 4); s[:, e] = v[1]
    return (c.reshape(128, -1), s)
def pk(c, s):
    return (np.ascontiguousarray(c), mx_ref.live(s))
def emit(q):
    return q[0], q[1]
def decode(q):
    o = []
    for b in range(4):
        e = np.zeros((128, 128, 4), np.float32); e[np.arange(128), np.arange(128), b] = 1
        o.append(mx_ref.matmul(mx_ref.quantize(e.reshape(128, 512).astype(BF)), q))
    return np.stack(o, axis=2).reshape(128, -1)
def f(rng, *shape):
    return mx_ref.flush((rng.standard_normal(shape, dtype=np.float32) * np.exp2(rng.integers(-2, 3, shape[:-1] + (1,)))).astype(BF))
def wide(rng, *shape, cols=0):
    v = rng.standard_normal(shape, dtype=np.float32) * np.exp2(rng.integers(-12, 13, shape)).astype(np.float32)
    if cols: v *= np.repeat(np.exp2(rng.integers(-cols, cols + 1, shape[:-2] + (1, shape[-1] // 4))) * (rng.random(shape[:-2] + (1, shape[-1] // 4)) > 0.0625), 4, axis=-1).astype(np.float32)
    return mx_ref.flush(v.astype(BF))
P, K, R, O = 192, 48, 2, 2
def big(v):
    v = v.astype(np.float32)
    v[np.abs(v) < np.float32(2.0 ** -16)] = 0
    return v.astype(BF)
def times(t, k):
    return mx_ref.flush((t.astype(np.float32) * np.float32(k)).astype(BF))
def signs(d, v, s):
    g = np.where(d["u"][0, :, :4].astype(np.float32) < 0, -1, 1)
    a = np.abs(v.astype(np.float32)).reshape(N, 128, -1, 4) * g[None, :, None, :] * s[:, None, :, None]
    return big(a.reshape(N, 128, -1))
def counted(rng, d):
    n = P // 2 + rng.permutation(K)[:N]
    return signs(d, d["tb"], np.stack([np.where(rng.permutation(P) < n[r], 1, -1) for r in range(N)]))
def setup_inputs(rng):
    v = np.zeros((128, 512), np.float32)
    v[:, :4] = f(rng, 128, 4).astype(np.float32)
    return {"tb": big(f(rng, N, 128, 4 * P)), "nz": big(f(rng, N, 128, 4 * R * K)), "u": np.stack([v.astype(BF)] * N), "w": f(rng, N, 128, 512 * O)}
def setup_inputs_down(rng):
    d = setup_inputs(rng)
    d["tb"] = counted(rng, d)
    d["nz"] = signs(d, 64 * (1 + rng.random((N, 128, 4 * R * K))), np.full((N, R * K), -1))
    return d
def setup_inputs_spread(rng):
    d = setup_inputs(rng)
    t, r = big(wide(rng, N, 128, 4 * P, cols=6)), int(rng.integers(0, N))
    x = (1 + rng.random((N, 128, 4 * P))) * np.exp2(rng.integers(12, 18, (N, 128, 4 * P)) + np.repeat(rng.integers(0, 4, (N, 1, P)), 4, axis=2))
    t[r] = signs(d, x, np.ones((N, P), np.int64))[r]
    return {**d, "tb": t, "nz": big(wide(rng, N, 128, 4 * R * K, cols=6)), "u": times(d["u"], 2.0 ** 24)}
def setup_inputs_swap(rng):
    d = setup_inputs(rng)
    d["tb"] = counted(rng, d)
    d["nz"] = signs(d, 64 * (1 + rng.random((N, 128, 4 * R * K))), np.full((N, R * K), 1))
    return d
def setup_inputs_ties(rng):
    d = setup_inputs(rng)
    a = rng.permutation(N) <= N // 2
    d["tb"] = np.stack([cols(d["tb"][int(a[r])], rng.permutation(P) % (P // (K + 1))) for r in range(N)])
    d["nz"] = np.stack([d["nz"][0]] * N)
    return d
def setup_inputs_zero(rng):
    d = setup_inputs(rng)
    d["u"] = times(np.abs(d["u"].astype(np.float32)), 2.0 ** -26)
    d["tb"], d["nz"] = big(times(d["tb"], 2.0 ** -10)), big(times(d["nz"], 2.0 ** -10))
    s, a = np.zeros((N, P), np.int64), rng.permutation(N)
    for i in range(N - 1):
        m, n, e = P // 2 - 4 * i, K // 2 - i, rng.permutation(P)
        s[a[i], e[:m]] = 1
        s[a[i], e[m:m + n]] = -1
    d["tb"] = signs(d, d["tb"], s)
    for r in range(N):
        d["tb"][r].reshape(128, P, 4)[:, np.flatnonzero(s[r] == 0)[1::2]] = BF(-0.0)
    d["nz"] = big(d["nz"].astype(np.float32) * np.repeat(rng.random((N, 1, R * K)) > 0.25, 4, axis=2))
    return d
def check_inputs(d):
    b = []
    for k, low, high in (("tb", -16, 26), ("nz", -16, 26), ("u", -30, 30), ("w", -30, 30)):
        v = np.abs(d[k].astype(np.float32))
        if not (np.isfinite(v).all() and ((v == 0) | (v >= 2.0 ** low) & (v <= 2.0 ** high)).all()): b.append("a value of " + k)
    v = d["u"].astype(np.float32)
    if (v[:, :, 4:] != 0).any(): b.append("u has numbers behind its column 0")
    if (v != v[:1]).any(): b.append("u isn't the same on all ranks")
    return b
def reference(tb, nz, u, w):
    T = [mx_ref.quantize(tb[r]) for r in range(N)]
    qu = [mx_ref.quantize(u[r]) for r in range(N)]
    od = np.zeros((N, R, N), np.float32)
    for t in range(R):
        s = [mx_ref.matmul(qu[r], T[r])[0] + np.float32(0) for r in range(N)]
        fitness = np.array([np.count_nonzero(s[r] > 0) for r in range(N)])
        place = np.argsort(-fitness, kind="stable")
        od[:, t] = place
        new = T[:]
        for i in range(N // 2):
            a, b = place[i], place[N - 1 - i]
            j = np.argsort(s[a], kind="stable")[:K]
            noise = mx_ref.quantize(np.ascontiguousarray(nz[b][:, 4 * t * K:4 * (t + 1) * K]))
            v = np.float32(0.5) * decode(pick(T[a], j)) + np.float32(0.5) * decode(noise)
            new[b] = put(T[a], j, mx_ref.quantize(np.ascontiguousarray(v.astype(BF))))
        T = new
    oc, osc, y = np.zeros((N, 128, 4 * P), np.uint8), np.zeros((N, 16, P), np.uint8), np.zeros((N, 128, O * P), np.float32)
    for r in range(N):
        oc[r], osc[r] = emit(T[r])
        for o in range(O):
            y[r, :, o * P:(o + 1) * P] = mx_ref.matmul(mx_ref.quantize(np.ascontiguousarray(cut(w[r], o))), T[r])
    return {"oc": oc, "osc": osc, "od": od, "y": y}

@@ -1,0 +1,598 @@
+from concourse.bass import DstId, RemoteDMATransfer
+from concourse.mybir import dt, AluOpType as O, AxisListType, ActivationFunctionType as F
+
+P, K, N = 192, 48, 6
+LX, HX, NX = 288, 576, 960
+TH = 96
+BIG = 1e29
+STEP = 2048.0
+
+SCRATCH = {"mdr": ("dram", [16, 48], "uint16")}
+ARENA = {}
+for _d, _l in (
+        ("bfloat16", "ut 4 tbt 768 nzt 704 wt 1024 ubt 512 onet 516 eht 516 vt 512 vn 768 ct 768 idt 128 x48 288 pos 288 psc 288"),
+        ("int32", "ipd 128 pi 2 pa 6 ia 32 hi 8 fb 16 hw 54"),
+        ("float32", "ir 800 m16 4 t16 192 dq 192 ones 128 paf 6 cn 16 bm 128 dm 32 nw 4 nws 4 nr8 8 "
+                    "rsq 32 c48 8 sm 128 sm1 64 sg 192 sg1 192 sc 192 prm 192 sc2 192 "
+                    "msgf 2 sw 968 dn 192 d0 192 d1 192 g2 192 g3 192 v1r 16 rke 16 cnx 12 n6 6 bzf 16 sgn 192 "
+                    "st 192 m32 32 sq 32 ysb 384 odt 16 rho 96 hq 16 ca 96 hb 96 hc 96 sb 96 sd 96 rg 96 pio 4"),
+        ("uint16", "land 48 v6 8 rw 54 l6 6 rof 12 ol 12 oll 4 om 4 ox 4 ob 6 zg 16 osl 16 oh 12 ofz 12 roc 12 ofin 12 pt 8")):
+    _w = _l.split()
+    for _k, _n in zip(_w[::2], _w[1::2]):
+        SCRATCH[_k] = ("sbuf", [128, int(_n)], _d)
+_w = ("tq 192 nq 176 wq 256 uq 128 oneq 128 eq 512 cq 192 ls 48 nb 192 hp 192 hs 192 lb 128 tz 192 xs 48 w0 1152 "
+      "fin 192").split()
+for _k, _n in zip(_w[::2], _w[1::2]):
+    SCRATCH[_k] = ("sbuf", [128, int(_n)], "float8_e4m3fn_x4")
+    SCRATCH[_k + "_s"] = ("sbuf", [128, int(_n)], "uint8")
+for _k in range(8):
+    SCRATCH["ps%d" % _k] = ("psum", [128, 512], "float32")
+_o = 0
+for _n, _l in ((54, "vf h2"), (96, "y0g yt"),
+               (16, "key ks zr0 zr1 wr0 wr1 wf wb wc cz fa b32 l16 dlt fl fm"),
+               (8, "gt pl t5 t0 apre fan r96 r144 u1 v1 c1 bz cb hb2 hc2 tk")):
+    for _k in _l.split():
+        ARENA[_k] = (_o, _n)
+        _o += _n + (-_n) % 8
+SCRATCH["ar"] = ("sbuf", [128, _o], "float32")
+
+DMAS = ["du", "dtb", "dnz", "dw", "dpv", "dpad", "dls", "dhb", "dmd", "drw", "dxs", "dout"]
+SEMAPHORES = ["cv", "ca", "ct", "cg", "am", "al", "ah", "ax", "an", "a3", "left"] + DMAS
+
+
+def r(name, a=0, b=None, step=1, p=0, q=128):
+    o, n = ARENA[name] if name in ARENA else (0, SCRATCH[name][1][1])
+    return ("ar" if name in ARENA else name, p, q, o + a, o + (n if b is None else b), step)
+
+
+def meet(x, y):
+    return (x[0] == y[0] and x[1] < y[2] and y[1] < x[2] and x[3] < y[4] and y[3] < x[4]
+            and not (x[5] == y[5] and (x[3] - y[3]) % x[5]))
+
+
+def covers(x, y):
+    return x[1] <= y[1] and y[2] <= x[2] and x[3] <= y[3] and y[4] <= x[4] and (x[5] == 1 or x[5] == y[5] and x[3] == y[3])
+
+
+def weave(*chains):
+    for k in range(max(len(c) for c in chains)):
+        for c in chains:
+            if k < len(c):
+                c[k]()
+
+
+def rank_program(g, core, T, topo):
+    me = T.rank_of(core)
+    if me is None:
+        return
+    queue = {"v": g.vector, "a": g.scalar, "t": g.tensor, "g": g, "s": g.sync}
+    V, A, X = g.vector, g.scalar, g.tensor
+    count = {"v": 0, "a": 0, "t": 0, "g": 0}
+    clk = {q: {} for q in queue}
+    snap, wr, rd, due = {}, {}, {}, {}
+
+    def wait(q, s, v):
+        if clk[q].get(s, 0) < v:
+            queue[q].wait_ge(T.sem[s], v)
+            for s2, v2 in snap.get((s, v), {}).items():
+                clk[q][s2] = max(clk[q].get(s2, 0), v2)
+            clk[q][s] = v
+
+    def before(q, reads, writes):
+        need = {}
+        for x in reads + writes:
+            bank = SCRATCH[x[0]][0] == "psum"
+            hits = [(y, tok) for y, tok in wr.get(x[0], ()) if meet(x, y) or bank and tok[0] != "c" + q]
+            if x in writes:
+                hits += [(y, tok) for y, tok in rd.get(x[0], ()) if meet(x, y) or bank and tok[0] != "c" + q]
+            elif bank:
+                hits += [(y, tok) for y, tok in rd.get(x[0], ()) if tok[0] != "c" + q]
+            for y, tok in hits:
+                need[tok[0]] = max(need.get(tok[0], 0), tok[1])
+        for s in sorted(need):
+            wait(q, s, need[s])
+
+    def wrote(x, tok):
+        for d in (wr, rd):
+            d[x[0]] = [e for e in d.get(x[0], ()) if not covers(x, e[0])]
+        wr[x[0]].append((x, tok))
+
+    def issue(q, reads, writes, fn, sem=None, total=0):
+        before(q, reads, writes)
+        if sem is None:
+            count[q] += 1
+            tok = ("c" + q, count[q])
+            fn().then_inc(T.sem[tok[0]], 1)
+            snap[tok] = dict(clk[q])
+        else:
+            tok = (sem, total)
+            fn().then_inc(T.sem[sem], 16)
+            due[sem] = total
+        for x in reads:
+            rd.setdefault(x[0], []).append((x, tok))
+        for x in writes:
+            wrote(x, tok)
+
+    def ap(x, bits=None):
+        v = T[x[0]][x[1]:x[2], x[3]:x[4]:x[5]] if x[5] > 1 else T[x[0]][x[1]:x[2], x[3]:x[4]]
+        return v.bitcast(bits or dt.uint8) if SCRATCH[x[0]][2] == "float8_e4m3fn_x4" else v
+
+    def mx(x):
+        return T[x[0]][:, x[3]:x[4]]
+
+    def num(s):
+        return ap(s) if isinstance(s, tuple) else s
+
+    def ts(out, in0, s1, op0, s2=None, op1=None):
+        rs = [in0] + [s for s in (s1, s2) if isinstance(s, tuple)]
+        if op1 is None:
+            issue("v", rs, [out], lambda: V.tensor_scalar(ap(out), ap(in0), num(s1), None, op0))
+        else:
+            issue("v", rs, [out], lambda: V.tensor_scalar(ap(out), ap(in0), num(s1), num(s2), op0, op1))
+
+    def tt(out, a, b, op, off=None):
+        if off is None:
+            issue("v", [a, b], [out], lambda: V.tensor_tensor(ap(out), ap(a), ap(b), op))
+        else:
+            issue("v", [a, b, off], [out], lambda: V.tensor_tensor(ap(out), ap(a).indirect(ap(off)), ap(b), op))
+
+    def cp(out, in_):
+        issue("v", [in_], [out], lambda: V.tensor_copy(ap(out), ap(in_)))
+
+    def ac(out, in_):
+        issue("a", [in_], [out], lambda: A.activation(ap(out), ap(in_), F.Copy))
+
+    def lin(out, in_, scale, bias, func=F.Identity):
+        rs = [in_] + ([bias] if isinstance(bias, tuple) else [])
+        issue("a", rs, [out], lambda: A.activation(ap(out), ap(in_), func, bias=num(bias), scale=scale))
+
+    def gather(out, win, off):
+        issue("v", [win, off], [out], lambda: V.tensor_copy(ap(out), ap(win).indirect(ap(off))))
+
+    def gather_a(out, win, off, scale=1.0):
+        issue("a", [win, off], [out], lambda: A.activation(ap(out), ap(win).indirect(ap(off)), F.Identity, scale=scale))
+
+    def scatter(win, val, off):
+        issue("v", [val, off], [win], lambda: V.tensor_copy(ap(win).indirect(ap(off)), ap(val)))
+
+    def scan(out, keep, add, op0=O.min, op1=O.add):
+        issue("v", [keep, add], [out], lambda: V.tensor_tensor_scan(ap(out), ap(keep), ap(add), 0.0, op0, op1))
+
+    corr = r("cn", 0, 1)
+
+    def select(out, val, a, b):
+        scan(out, r("dq", a, b), val, O.add, O.max)
+
+    def fill(x, c):
+        issue("v", [], [x], lambda: V.memset(ap(x), c))
+
+    def zero(x, src):
+        lin(x, src, 0.0, 0.0)
+
+    def both(name, a, b):
+        return [r(name, a, b), r(name + "_s", a, b)]
+
+    def qz(cod, o, n, tile):
+        c, s = both(cod, o, o + n)
+        issue("v", [tile], [c, s], lambda: V.quantize_mx(mx(c), mx(s), ap(tile)))
+
+    def mm(k, lhs, lo, rhs, ro, n, start=True, stop=True):
+        w, x, out = both(lhs, lo, lo + 128), both(rhs, ro, ro + n), r("ps%d" % k, 0, n)
+        issue("t", w + x, [out], lambda: X.matmul_mx(ap(out), mx(w[0]), mx(w[1]), mx(x[0]), mx(x[1]), start, stop))
+
+    def pick(dst, c, n, src, a, b, off, parts):
+        do, so, wc, ws = r(dst, c, c + n), r(dst + "_s", c, c + n), r(src, a, b), r(src + "_s", a, b)
+        issue("v", [r(src, x, y) for x, y in parts] + [off], [do], lambda: V.tensor_copy(
+            ap(do, dt.uint32), ap(wc, dt.uint32).indirect(ap(off))))
+        issue("a", [r(src + "_s", x, y) for x, y in parts] + [off], [so], lambda: A.activation(
+            ap(so), ap(ws).indirect(ap(off)), F.Copy))
+
+    def iota(x, pattern, base, cm):
+        if SCRATCH[x[0]][2] == "int32":
+            issue("g", [], [x], lambda: g.iota(ap(x), pattern, base, cm))
+        else:
+            issue("g", [], [x], lambda: g.iota(ap(x), pattern, base, cm, allow_small_or_imprecise_dtypes=True))
+
+    def dma(q, out, in_, sem, total=16):
+        issue(q, [in_] if isinstance(in_, tuple) else [], [out] if isinstance(out, tuple) else [],
+              lambda: queue[q].dma_start(num(out), num(in_)), sem, total)
+
+    def move(dst, a, src, b, n, sem, total=32):
+        for x, y in zip(both(dst, a, a + n), both(src, b, b + n)):
+            dma("s", x, y, sem, total)
+
+    def idle():
+        pass
+
+    sh = me % 2
+    e6, em = (sh, sh + 6), me + sh
+
+    others = [x for x in range(N) if x != me]
+
+    def far_of(x):
+        return [y for y in range(N) if topo.chip(T.cores[y]) != topo.chip(T.cores[x])]
+    far = far_of(me)
+    near = [x for x in others if x not in far]
+    all_eng = topo.engines(core, T.cores[near[0]])
+    out_eng = topo.engines(core, T.cores[far[0]])
+    in_eng = [e for e in all_eng if e not in out_eng]
+
+    def third(x):
+        return [y for y in range(N) if y not in far_of(x)].index(x)
+    mate = [x for x in far if third(x) == third(me)][0]
+
+    def mask(es):
+        return sum(1 << e for e in es)
+
+    def dst(x):
+        a = topo.addr(T.cores[x])
+        return DstId(rid=a[0], pnc=a[1])
+
+    def send(transfers, src):
+        before("g", [src], [])
+        due["left"] = due.get("left", 0) + sum(len(e[1]) for e in transfers)
+        g.remote_dma_fused([RemoteDMATransfer(dst_ids=[dst(y) for y in x], dma_engine_mask=mask(es), remote_sem=T.sem[sem],
+                                              srcs=[ap(s)], dsts=[ap(to)] * len(x)) for x, es, s, to, sem in transfers],
+                           local_sem=T.sem["left"])
+
+    def spread(src, to, sem, sem2=None):
+        send([(far, out_eng, src, to, sem), (near, in_eng, src, to, sem2 or sem)], src)
+
+    h_all = len(all_eng) // 2
+    n_all = sum(len(out_eng) if x in far else len(in_eng) for x in others)
+    for sem, tot, whom, buf, base, w in (("al", 2 * n_all, others, "w0", lambda x: K * x, K),
+                                         ("ax", 2 * len(out_eng) * len(far), far, "w0", lambda x: LX + K * x, K),
+                                         ("an", 2 * len(in_eng) * len(near), near, "w0", lambda x: LX + K * x, K),
+                                         ("ah", 2 * len(out_eng), [mate], "hp", lambda x: TH, TH),
+                                         ("a3", 2 * h_all * len(near), near, "w0", lambda x: HX + TH * third(x), TH)):
+        due[sem] = tot
+        for x in whom:
+            for e in both(buf, base(x), base(x) + w):
+                wrote(e, (sem, tot))
+    due["am"] = n_all
+    for x in others:
+        wrote(r("land", 8 * x, 8 * x + 1), ("am", n_all))
+
+    dma("s", r("ut"), T.u[:, 0:4], "du")
+    dma("s", r("tbt"), T.tb[:, :], "dtb")
+    dma("s", r("nzt", 0, 384), T.nz[:, :], "dnz", 32)
+    dma("s", r("nzt", 384, 704), T.nz[:, 0:320], "dnz", 32)
+    dma("s", r("vt", 192, 512), T.tb[:, 0:320], "dpv")
+    dma("s", r("wt"), T.w[:, :], "dw")
+
+    iota(r("pi"), [[0, 2]], 0, 1)
+    iota(r("ipd"), [[1, 128]], 0, -1)
+    iota(r("t16"), [[0, 12], [1, 16]], 0, 0)
+    iota(r("ir", 0, 192), [[1, 192]], 0, 0)
+    iota(r("m16"), [[16, 4]], 0, 0)
+    iota(r("n6"), [[16, 6]], 0, 0)
+    iota(r("c48"), [[48, 8]], 0, 0)
+    iota(r("rke"), [[1, 16]], -sh, 0)
+    iota(r("cnx"), [[16, 12]], NX, 0)
+    iota(r("ir", 192, 800), [[1, 608]], 192, 0)
+    iota(r("x48"), [[0, 6], [1000, 48]], 0, 0)
+
+    fill(r("ones"), 1.0)
+    fill(r("onet"), 1.0)
+    zero(r("ct", 0, 512), r("onet", 0, 512))
+    ts(r("pa", 0, 2), r("pi"), 64, O.bitwise_and)
+    ts(r("pa", 2, 4), r("pi"), 4, O.arith_shift_right)
+    ts(r("pa", 4, 6), r("pi"), 15, O.bitwise_and)
+    qz("oneq", 0, 128, r("onet", 0, 512))
+    cp(r("paf"), r("pa"))
+    own = r("paf", 4, 5)
+    ts(r("bm"), r("ipd"), 0.0, O.is_le, 3e29, O.mult)
+    for k, (a, b) in enumerate(((7.5, 1.0), (11.5, -5.0), (12.5, 4.0))):
+        ts(r("pio", k, k + 1), own, a, O.is_gt, b, O.mult)
+    for k in range(3):
+        tt(r("pio", 3, 4), r("pio", k, k + 1), r("pio", 3, 4) if k else own, O.add)
+    for k in range(4):
+        if k % 2:
+            lin(r("ubt", k, 512, 4), r("ones"), 0.0, r("ut", k, k + 1))
+        else:
+            ts(r("ubt", k, 512, 4), r("onet", 0, 128), r("ut", k, k + 1), O.mult)
+    zero(r("ct", 512, 768), r("onet", 0, 256))
+    lin(r("t16", 0, 192, 16), r("ones", 0, 12), 0.0, -1000.0)
+    lin(r("cn", 1, 2), own, 1.0, 0.5)
+    lin(corr, own, 32.0, -480.0, F.Square)
+    lin(r("cn", 10, 11), r("paf", 0, 1), -4.0, 256.0)
+    lin(r("cn", 11, 12), r("paf", 0, 1), 4.0, 0.0)
+    zero(r("eht"), r("onet"))
+    qz("uq", 0, 128, r("ubt"))
+
+    qz("tq", 0, 192, r("tbt"))
+    mm(0, "uq", 0, "tq", 0, 192)
+    mm(1, "tq", 0, "uq", 0, 128)
+    mm(2, "tq", 64, "uq", 0, 128)
+    mm(6, "uq", 0, "tq", 0, 192)
+    ts(r("dq"), r("t16"), r("cn", 1, 2), O.subtract, STEP, O.mult)
+    move("lb", K, "tq", K, 80, "dpad", 32)
+
+    lin(r("sg"), r("ps6", 0, 192), 1.0, 0.0, F.Sign)
+    issue("a", [r("sg")], [r("sg1"), r("msgf", 0, 1)], lambda: A.activation(
+        ap(r("sg1")), ap(r("sg")), F.Relu, accum_out=ap(r("msgf", 0, 1))))
+
+    def lower(src, a=0, b=192):
+        return r(src, a, b, 1, 64, 128)
+
+    def gt_ops(src, sp0, sp1):
+        return [lambda: ts(r("ct", 0, 512, 4), r(src, 0, 128), sp0, O.is_gt),
+                lambda: ts(r("ct", 512, 768, 4), r(src, 128, 192), sp0, O.is_ge),
+                lambda: ts(r("ct", 1, 768, 4, 64), lower(src), sp1, O.is_gt)]
+
+    def tie0(sp0):
+        ts(r("ct", 2, 512, 4), r("sm"), sp0, O.is_equal)
+
+    def low1(src):
+        tt(r("sm1", 0, 64, 1, 64), lower(src, 128), r("bm", 64, 128, 1, 64), O.add)
+
+    def tie1(sp1):
+        ts(r("ct", 515, 768, 4, 64), r("sm1", 0, 64, 1, 64), sp1, O.is_equal)
+
+    def rank_ops():
+        qz("cq", 0, 192, r("ct"))
+        mm(3, "oneq", 0, "cq", 0, 192)
+
+    def order_ops(out, a, b):
+        return [lambda: select(r("sc2", a, b), r("prm", a, b), a, b),
+                lambda: ts(out, r("sc2", a + 15, b, 16), corr, O.subtract)]
+
+    s0, s1 = r("ps1", 0, 1), r("ps2", 0, 1, 1, 64)
+    gts = gt_ops("ps0", s0, s1)
+    tt(r("sm"), r("ps0", 0, 128), r("bm"), O.add)
+    low1("ps0")
+    gts[0]()
+    tie0(s0)
+    gts[1]()
+    gts[2]()
+    tie1(s1)
+    rank_ops()
+    mm(4, "cq", 0, "oneq", 0, 128)
+    mm(5, "cq", 64, "oneq", 0, 128)
+    ts(r("idt"), r("ipd"), 0.0, O.is_equal, 0.5, O.mult)
+    ac(r("eht", 3, 515, 4), r("idt"))
+
+    my_land = r("land", 8 * me, 8 * me + 1)
+    select(r("sc"), r("ps3", 0, 192), 0, 192)
+    ts(r("msgf", 1, 2), r("msgf", 0, 1), r("cn", 10, 11), O.mult, r("ps4", 0, 1), O.add)
+    ts(r("rof"), r("sc", 15, 192, 16), corr, O.subtract)
+    ts(my_land, r("ps5", 0, 1), r("cn", 11, 12), O.mult, r("msgf", 1, 2), O.add)
+    spread(my_land, my_land, "am")
+    scatter(r("prm"), r("ir", 0, 192), r("rof"))
+    weave(order_ops(r("ol", 0, 3), 0, 48))
+    pick("ls", 0, 48, "tq", 0, 192, r("ol", 0, 3), [(0, 192)])
+    for x, y in zip(both("ls", 0, K), both("w0", K * me, K * me + K)):
+        spread(x, y, "al")
+    move("w0", K * me, "ls", 0, K, "dls")
+
+    six = (0, 6)
+    lin(r("nr8", *six), r("ir", *six), -0.125, 0.0)
+    lin(r("key"), r("ones", 0, 16), 0.0, -100.0)
+    lin(r("cn", 2, 3), own, 1.0, -6.0, F.Relu)
+    lin(r("nw", 0, 3), r("m16", 0, 3), 1.0, own)
+    lin(r("nws", 0, 3), r("nw", 0, 3), 1.0 / K, 0.0)
+    weave([lambda: fill(r("fb"), 0)], order_ops(r("om", 0, 3), 48, 96),
+          [idle, lambda: qz("nq", 0, 176, r("nzt"))])
+    pick("nb", 0, 48, "tq", 0, 192, r("om", 0, 3), [(0, 192)])
+    lin(r("cn", 4, 5), own, 6.0, 0.0)
+    lin(r("v1r"), r("rke"), 16.0, r("pio", 3, 4))
+    lin(r("cn", 6, 7), corr, 1.0, float(K))
+    lin(r("cn", 7, 8), r("ones", 0, 1), 0.0, 0.5 - K)
+    lin(r("cn", 8, 9), r("ones", 0, 1), 0.0, 0.5 - 2 * K)
+    lin(r("cn", 9, 10), r("pio", 3, 4), 1.0, 16.0 * me)
+    zero(r("hq"), r("ones", 0, 16))
+    for x in range(N):
+        lin(r("hq", x + sh, x + sh + 1), r("ones", 0, 1), 0.0, float(HX + TH * (3 if x == mate else third(x)) - 2 * K))
+    lin(r("cnx"), r("cnx"), 1.0, own)
+    lin(r("rho", 84, 96), r("ones", 0, 12), 0.0, 0.0)
+    lin(r("rsq"), r("x48", 0, 32), 0.0, 1.0)
+    lin(r("rsq", 0, 32, 16), r("ones", 0, 2), 0.0, 0.0)
+    lin(r("sw", HX, NX + 8), r("ir", 0, 392), 0.0, BIG)
+
+    def unit(k):
+        qz("eq", 128 * k, 128, r("eht", 3 - k, 515 - k))
+
+    def noise(t, stop):
+        for k in range(4):
+            mm(4 + k, "eq", 128 * k, "nq", K * t, 128, True, stop)
+
+    def places(k, val, zr):
+        pu, tpu = r("pt", 4 * k, 4 * k + 1), r("pt", 4 * k + 2, 4 * k + 3)
+        pl, t5 = r("pl", k, k + 1), r("t5", k, k + 1)
+        select(r("ks"), r("key"), 0, 16)
+        ts(r("gt", *six), r("key", *e6), corr, O.add, r("ks", 15, 16), O.is_gt)
+        issue("v", [r("gt", *six)], [pl], lambda: V.tensor_reduce(ap(pl), ap(r("gt", *six)), AxisListType.X, O.add))
+        ts(pu, pl, r("cn", 2, 3), O.add)
+        ts(t5, pl, -1.0, O.mult, 5.0, O.add)
+        scatter(r("wr%d" % k), val, pu)
+        ts(tpu, t5, pl, O.min)
+        if k:
+            scatter(r("wb"), r("b32"), pu)
+        gather(zr, r("wr%d" % k), tpu)
+        return pu, tpu
+
+    def note(k, scale):
+        lin(r("odt", 6 * k, 6 * k + 6), r("wr%d" % k, *six), scale, 0.0)
+
+    def anew(buf, off, parts, end):
+        pick(buf, 0, 48, "w0", 0, end, off, parts)
+        for k in range(4):
+            mm(4 + k, "eq", 128 * k, buf, 0, 128, False, True)
+
+    def pack_ops(out, o):
+        return [lambda k=k: (cp if k % 2 else ac)(r("vt", k, 192, 4), r("ps%d" % (4 + k), 0, 48)) for k in range(4)] + [
+            lambda: qz(out, o, 128, r("vt"))]
+
+    unit(0)
+    unit(1)
+    unit(2)
+    cp(r("l6"), r("ir", *six))
+    ts(r("ia"), r("ipd", 0, 32), 15, O.bitwise_and)
+    ts(r("dm"), r("ia"), 0.0, O.is_equal)
+    ts(r("hi", *six), r("land", 0, 48, 8), 1.0 / 256, O.mult, -127.5 / 256, O.add)
+    issue("g", [r("hi", *six)], [r("fb", *e6)], lambda: g.partition_broadcast(
+        ap(r("fb", *e6)), ap(r("hi", 0, 6, 1, 0, 1)), 128))
+    cp(r("v6", *six), r("land", 0, 48, 8))
+    unit(3)
+    noise(0, False)
+    tt(r("key", *e6), r("fb", *e6), r("nr8", *six), O.add)
+    pu, tpu = places(0, r("rke"), r("zr0"))
+    ts(r("oll", 0, 3), r("nws", 0, 3), r("zr0", em, em + 1), O.add, float(K), O.mult)
+    cp(r("rw", 48, 54), r("v6", *six))
+
+    for k in range(8):
+        dma("s", ("mdr", 0, 16, 6 * k, 6 * k + 6, 1), r("v6", 0, 6, 1, 16 * k, 16 * k + 16), "dmd", 128)
+    for k in range(8):
+        dma("s", r("rw", 0, 48, 1, 16 * k, 16 * k + 16), ("mdr", 0, 16, 0, 48, 1), "drw", 128)
+
+    note(0, 1.0)
+    ts(r("tk", 0, 1), r("zr0", em, em + 1), float(me), O.not_equal, 64.0, O.mult)
+    scatter(r("wf"), r("fb"), pu)
+    ts(r("ox", 0, 3), r("nw", 0, 3), r("tk", 0, 1), O.add)
+    anew("lb", r("oll", 0, 3), [(0, 288)], 288)
+    gather(r("fa"), r("wf"), tpu)
+    scatter(r("wc"), r("hq"), pu)
+    tt(r("t0", *six), r("zr0", *e6), r("ir", *six), O.not_equal)
+    gather(r("cz"), r("wc"), tpu)
+    weave(pack_ops("nb", 64))
+    pick("xs", 0, 48, "nb", 0, 192, r("ox", 0, 3), [(0, 48), (64, 192)])
+    for x, y in zip(both("xs", 0, K), both("w0", LX + K * me, LX + K * me + K)):
+        spread(x, y, "ax", "an")
+    move("w0", LX + K * me, "xs", 0, K, "dxs")
+    noise(1, True)
+    for k in range(4):
+        ac(r("dn", K * k, K * k + K), r("ps%d" % (4 + k), 0, K))
+    weave(order_ops(r("ol", 6, 12), 96, 192), [lambda: ts(r("ob"), r("zr0", *e6), r("cn", 4, 5), O.add)])
+    pick("hp", 0, TH, "tq", 0, 192, r("ol", 6, 12), [(0, 192)])
+    for x, y in zip(both("hp", 0, TH), both("hp", TH, 2 * TH)):
+        send([([mate], out_eng, x, y, "ah")], x)
+    move("w0", HX + TH * third(me), "hp", 0, TH, "dhb", 64)
+    move("w0", HX + TH * 3, "hp", TH, TH, "dhb", 64)
+    mm(1, "uq", 0, "w0", 0, 288)
+    qz("wq", 0, 256, r("wt"))
+
+    fit = [
+        lambda: lin(r("r96", *six), r("fa", *e6), 1.0, float(K - P + K), F.Relu),
+        lambda: lin(r("r144", *six), r("fa", *e6), 1.0, float(K - P), F.Relu),
+        lambda: tt(r("fan", *six), r("fa", *e6), r("nr8", *six), O.add),
+        lambda: tt(r("u1", *six), r("r96", *six), r("r144", *six), O.subtract),
+        lambda: tt(r("v1", *six), r("u1", *six), r("r144", *six), O.subtract),
+        lambda: tt(r("fan", *six), r("fan", *six), r("u1", *six), O.subtract),
+        lambda: tt(r("v1", *six), r("v1", *six), r("t0", *six), O.mult),
+        lambda: tt(r("apre", *six), r("fan", *six), r("v1", *six), O.add)]
+    bases = [
+        lambda: lin(r("c1", *six), r("t0", *six), float(LX), 0.0),
+        lambda: lin(r("bz", *six), r("zr0", *e6), float(K), float(LX - K)),
+        lambda: tt(r("c1", *six), r("c1", *six), r("c48", *six), O.add),
+        lambda: tt(r("hc2", *six), r("cz", *e6), r("bz", *six), O.subtract),
+        lambda: tt(r("hb2", *six), r("bz", *six), r("c1", *six), O.subtract),
+        lambda: tt(r("cb", *six), r("cz", *e6), r("c1", *six), O.add),
+        lambda: gather_a(r("hc"), r("hc2"), r("l6"), 0.5),
+        lambda: gather_a(r("hb"), r("hb2"), r("l6"), 0.5),
+        lambda: gather_a(r("ca"), r("cb"), r("l6"), 0.5),
+        lambda: ts(r("bzf"), r("zr0"), *((min(far) - 0.5, O.is_gt) if me < min(far) else (max(far) + 0.5, O.is_lt)), TH, O.mult),
+        lambda: lin(r("b32"), r("bzf"), 1.0, own),
+        lambda: ac(r("sw", 0, 288), r("ps1", 0, 288))]
+    where = [
+        lambda: ts(r("hw"), r("rw"), 1.0 / 256, O.mult, -127.5 / 256, O.add),
+        lambda: cp(r("vf"), r("rw")),
+        lambda: ts(r("h2"), r("hw"), -256.0, O.mult),
+        lambda: cp(r("rho", 54, 84), r("hw", 24, 54)),
+        lambda: tt(r("rho", 0, 54), r("h2"), r("vf"), O.add),
+        lambda: gather_a(r("rg"), r("rho"), r("ob")),
+        lambda: tt(r("yt"), r("rho"), r("ca"), O.add, r("ob")),
+        lambda: lin(r("sb"), r("rg"), 1.0, r("cn", 7, 8), F.Sign),
+        lambda: lin(r("sd"), r("rg"), 1.0, r("cn", 8, 9), F.Sign),
+        lambda: tt(r("sb"), r("sb"), r("hb"), O.mult),
+        lambda: tt(r("sd"), r("sd"), r("hc"), O.mult),
+        lambda: tt(r("yt"), r("yt"), r("sb"), O.add),
+        lambda: tt(r("y0g"), r("yt"), r("sd"), O.add)]
+    weave(bases, fit)
+    weave(where)
+
+    chip = min([me] + near)
+    for k, a in ((0, K * chip), (2, K * min(far))):
+        mm(k, "uq", 0, "w0", LX + a, 144)
+        ts(r("pos", a, a + 144), r("ps%d" % k, 0, 144), 0.0, O.is_gt)
+        ac(r("sw", LX + a, LX + a + 144), r("ps%d" % k, 0, 144))
+        scan(r("psc", a, a + 144), r("x48", a, a + 144), r("pos", a, a + 144))
+    tt(r("key", *e6), r("psc", 47, 288, 48), r("apre", *six), O.add)
+    pu, tpu = places(1, r("v1r"), r("zg"))
+    og, ofs = r("zg", em, em + 1), r("osl", 0, 12)
+    gather(r("bzf"), r("wb"), tpu)
+    gather(r("osl"), r("y0g"), og)
+
+    def holder(i):
+        x = near[i] + sh
+        ts(r("oh", 6 * i, 6 * i + 6), r("n6"), r("bzf", x, x + 1), O.add)
+    holder(0)
+    tt(r("m32"), r("sw"), r("dm"), O.mult, r("osl", 12, 14))
+    gather_a(r("st"), r("sw"), ofs)
+    gather_a(r("l16"), r("y0g"), og)
+    holder(1)
+    scan(r("sq"), r("rsq"), r("m32"), O.mult)
+    s0, s1 = r("sq", 15, 16), r("sq", 31, 32, 1, 64)
+
+    pick("hs", 0, 2 * TH, "hp", 0, 192, r("oh"), [(0, 192)])
+    for x, y in zip(("hs", "hs_s"), both("w0", HX + TH * third(me), HX + TH * third(me) + TH)):
+        send([([z], all_eng[h_all * i:h_all * i + h_all], r(x, TH * i, TH * i + TH), y, "a3") for i, z in enumerate(near)],
+             r(x))
+
+    tt(r("sm"), r("st", 0, 128), r("bm"), O.add)
+    lin(r("sgn", 0, 192, 1, 64), lower("st"), -1.0, s1, F.Sign)
+    lin(r("ct", 1, 768, 4, 64), r("sgn", 0, 192, 1, 64), -1.0, 0.0, F.Relu)
+    gts = gt_ops("st", s0, s1)
+    low1("st")
+    tie0(s0)
+    gts[0]()
+    gts[1]()
+    tie1(s1)
+    ts(r("ofz"), ofs, float(HX - 1), O.min)
+    rank_ops()
+
+    pick("tz", 0, 192, "w0", 0, 576, r("ofz"), [(0, 576)])
+    note(1, 1.0 / 16)
+    for k in range(4):
+        mm(4 + k, "eq", 128 * k, "tz", 0, 192)
+    for k in range(2):
+        ac(r("d%d" % k), r("ps%d" % (4 + k), 0, 192))
+    select(r("sc"), r("ps3", 0, 192), 0, 192)
+    ts(r("tk", 0, 1), r("zg", em, em + 1), r("cn", 9, 10), O.not_equal)
+    ts(r("roc"), r("sc", 15, 192, 16), corr, O.subtract, K - 1.0, O.min)
+    tt(r("dlt", 0, 12), r("cnx"), r("l16", 0, 12), O.subtract)
+    ts(r("fm", 0, 12), r("sc", 15, 192, 16), r("cn", 6, 7), O.is_lt, r("tk", 0, 1), O.mult)
+    for k in (2, 3):
+        gather_a(r("g%d" % k), r("dn", K * k, K * k + K), r("roc"))
+
+    def make(k):
+        if k < 2:
+            tt(r("vn", k, 768, 4), r("dn", K * k, K * k + K), r("d%d" % k), O.add, r("roc"))
+        else:
+            tt(r("vn", k, 768, 4), r("ps%d" % (4 + k), 0, 192), r("g%d" % k), O.add)
+    make(0)
+    tt(r("fl", 0, 12), r("fm", 0, 12), r("dlt", 0, 12), O.mult)
+    make(1)
+    tt(r("fl", 0, 12), r("fl", 0, 12), r("l16", 0, 12), O.add)
+    make(2)
+    make(3)
+    cp(r("ofin"), r("fl", 0, 12))
+    qz("w0", NX, 192, r("vn"))
+    pick("fin", 0, 192, "w0", 0, 1152, r("ofin"), [(0, 1152)])
+
+    dma("s", T.oc[:, :], r("fin"), "dout", 128)
+    mm(1, "wq", 0, "fin", 0, 192)
+    mm(2, "wq", 128, "fin", 0, 128)
+    mm(3, "wq", 128, "fin", 64, 128)
+    for k in range(4):
+        dma("s" if k < 2 else "a", T.osc[4 * k:4 * k + 4, :], r("fin_s", 0, 192, 1, 32 * k, 32 * k + 4), "dout", 128)
+    cp(r("ysb", 0, 192), r("ps1", 0, 192))
+    dma("s", T.y[:, 0:192], r("ysb", 0, 192), "dout", 128)
+    ac(r("ysb", 192, 320), r("ps2", 0, 128))
+    cp(r("ysb", 320, 384), r("ps3", 64, 128))
+    dma("a", T.y[:, 192:384], r("ysb", 192, 384), "dout", 128)
+    dma("s", T.od[:, :], r("odt", 0, 12, 1, 0, 1), "dout", 128)
+
+    for q in count:
+        due["c" + q] = count[q]
+    for s in sorted(due):
+        g.wait_ge(T.sem[s], due[s])

@@ -1,5 +1,5 @@
 from concourse.bass import DstId, RemoteDMATransfer
-from concourse.mybir import dt, AluOpType as O, AxisListType, ActivationFunctionType as F
+from concourse.mybir import dt, AluOpType as O, ActivationFunctionType as F
 
 P, K, N = 192, 48, 6
 LX, HX, NX = 288, 576, 960
@@ -10,17 +10,18 @@ STEP = 2048.0
 SCRATCH = {"mdr": ("dram", [16, 48], "uint16")}
 ARENA = {}
 for _d, _l in (
-        ("bfloat16", "ut 4 tbt 768 nzt 704 wt 1024 ubt 512 onet 516 eht 516 vt 512 vn 768 ct 768 idt 128 x48 288 pos 288 psc 288"),
+        ("bfloat16", "ut 4 tbt 768 nzt 704 wt 1024 ubt 512 onet 516 eht 516 vt 512 vn 768 ct 768 idt 128 x48 288 pos 288 psc 288 "
+                     "wct 1024 irb 192"),
         ("int32", "ipd 128 pi 2 pa 6 ia 32 hi 8 fb 16 hw 54"),
-        ("float32", "ir 800 m16 4 t16 192 dq 192 ones 128 paf 6 cn 16 bm 128 dm 32 nw 4 nws 4 nr8 8 "
-                    "rsq 32 c48 8 sm 128 sm1 64 sg 192 sg1 192 sc 192 prm 192 sc2 192 "
+        ("float32", "ir 8 m16 4 t16 192 dq 192 ones 128 paf 6 cn 24 bm 128 dm 32 nw 4 nws 4 nr8 8 "
+                    "rsq 32 c48 8 sm 128 sm1 64 sg 192 sg1 192 sc 192 sc2 192 "
                     "msgf 2 sw 968 dn 192 d0 192 d1 192 g2 192 g3 192 v1r 16 rke 16 cnx 12 n6 6 bzf 16 sgn 192 "
                     "st 192 m32 32 sq 32 ysb 384 odt 16 rho 96 hq 16 ca 96 hb 96 hc 96 sb 96 sd 96 rg 96 pio 4"),
-        ("uint16", "land 48 v6 8 rw 54 l6 6 rof 12 ol 12 oll 4 om 4 ox 4 ob 6 zg 16 osl 16 oh 12 ofz 12 roc 12 ofin 12 pt 8")):
+        ("uint16", "land 48 v6 8 rw 54 l6 6 ol 12 oll 4 om 4 ox 4 ob 6 zg 16 osl 16 oh 12 ofz 12 roc 12 ofin 12 pt 8")):
     _w = _l.split()
     for _k, _n in zip(_w[::2], _w[1::2]):
         SCRATCH[_k] = ("sbuf", [128, int(_n)], _d)
-_w = ("tq 192 nq 176 wq 256 uq 128 oneq 128 eq 512 cq 192 ls 48 nb 192 hp 192 hs 192 lb 128 tz 192 xs 48 w0 1152 "
+_w = ("tq 192 nq 176 wq 256 uq 128 oneq 384 eq 512 cq 192 ls 48 nb 192 hp 192 hs 192 lb 128 tz 192 xs 48 w0 1152 "
       "fin 192").split()
 for _k, _n in zip(_w[::2], _w[1::2]):
     SCRATCH[_k] = ("sbuf", [128, int(_n)], "float8_e4m3fn_x4")
@@ -29,8 +30,8 @@ for _k in range(8):
     SCRATCH["ps%d" % _k] = ("psum", [128, 512], "float32")
 _o = 0
 for _n, _l in ((54, "vf h2"), (96, "y0g yt"),
-               (16, "key ks zr0 zr1 wr0 wr1 wf wb wc cz fa b32 l16 dlt fl fm"),
-               (8, "gt pl t5 t0 apre fan r96 r144 u1 v1 c1 bz cb hb2 hc2 tk")):
+               (16, "key ks zr0 zr1 wr0 wr1 wf wb wc cz fa b32 l16 fl fm"),
+               (8, "gt pl t5 t0 k2 nc8 ap3 fan r96 r144 u1 v1 c1 bz cb hb2 hc2 tk")):
     for _k in _l.split():
         ARENA[_k] = (_o, _n)
         _o += _n + (-_n) % 8
@@ -78,7 +79,7 @@ def rank_program(g, core, T, topo):
                 clk[q][s2] = max(clk[q].get(s2, 0), v2)
             clk[q][s] = v
 
-    def before(q, reads, writes):
+    def before(q, reads, writes, adds=False):
         need = {}
         for x in reads + writes:
             bank = SCRATCH[x[0]][0] == "psum"
@@ -88,6 +89,8 @@ def rank_program(g, core, T, topo):
             elif bank:
                 hits += [(y, tok) for y, tok in rd.get(x[0], ()) if tok[0] != "c" + q]
             for y, tok in hits:
+                if bank and adds and tok[0] == "c" + q:
+                    continue
                 need[tok[0]] = max(need.get(tok[0], 0), tok[1])
         for s in sorted(need):
             wait(q, s, need[s])
@@ -97,8 +100,8 @@ def rank_program(g, core, T, topo):
             d[x[0]] = [e for e in d.get(x[0], ()) if not covers(x, e[0])]
         wr[x[0]].append((x, tok))
 
-    def issue(q, reads, writes, fn, sem=None, total=0):
-        before(q, reads, writes)
+    def issue(q, reads, writes, fn, sem=None, total=0, adds=False):
+        before(q, reads, writes, adds)
         if sem is None:
             count[q] += 1
             tok = ("c" + q, count[q])
@@ -178,7 +181,8 @@ def rank_program(g, core, T, topo):
 
     def mm(k, lhs, lo, rhs, ro, n, start=True, stop=True):
         w, x, out = both(lhs, lo, lo + 128), both(rhs, ro, ro + n), r("ps%d" % k, 0, n)
-        issue("t", w + x, [out], lambda: X.matmul_mx(ap(out), mx(w[0]), mx(w[1]), mx(x[0]), mx(x[1]), start, stop))
+        issue("t", w + x, [out], lambda: X.matmul_mx(ap(out), mx(w[0]), mx(w[1]), mx(x[0]), mx(x[1]), start, stop),
+              adds=not start)
 
     def pick(dst, c, n, src, a, b, off, parts):
         do, so, wc, ws = r(dst, c, c + n), r(dst + "_s", c, c + n), r(src, a, b), r(src + "_s", a, b)
@@ -253,23 +257,26 @@ def rank_program(g, core, T, topo):
     for x in others:
         wrote(r("land", 8 * x, 8 * x + 1), ("am", n_all))
 
-    dma("s", r("ut"), T.u[:, 0:4], "du")
+    dma("a", r("ut"), T.u[:, 0:4], "du")
     dma("s", r("tbt"), T.tb[:, :], "dtb")
     dma("s", r("nzt", 0, 384), T.nz[:, :], "dnz", 32)
     dma("s", r("nzt", 384, 704), T.nz[:, 0:320], "dnz", 32)
     dma("s", r("vt", 192, 512), T.tb[:, 0:320], "dpv")
     dma("s", r("wt"), T.w[:, :], "dw")
 
+    six = (0, 6)
     iota(r("pi"), [[0, 2]], 0, 1)
     iota(r("ipd"), [[1, 128]], 0, -1)
     iota(r("t16"), [[0, 12], [1, 16]], 0, 0)
-    iota(r("ir", 0, 192), [[1, 192]], 0, 0)
+    iota(r("irb"), [[1, 192]], 0, 0)
+    iota(r("ir"), [[1, 8]], 0, 0)
+    iota(r("hq"), [[0, 16]], 0, 0)
     iota(r("m16"), [[16, 4]], 0, 0)
     iota(r("n6"), [[16, 6]], 0, 0)
     iota(r("c48"), [[48, 8]], 0, 0)
     iota(r("rke"), [[1, 16]], -sh, 0)
     iota(r("cnx"), [[16, 12]], NX, 0)
-    iota(r("ir", 192, 800), [[1, 608]], 192, 0)
+    iota(r("hq", *e6), [[0, N // len(far)], [TH, len(far)]], HX - 2 * K, 0)
     iota(r("x48"), [[0, 6], [1000, 48]], 0, 0)
 
     fill(r("ones"), 1.0)
@@ -284,20 +291,20 @@ def rank_program(g, core, T, topo):
     ts(r("bm"), r("ipd"), 0.0, O.is_le, 3e29, O.mult)
     for k, (a, b) in enumerate(((7.5, 1.0), (11.5, -5.0), (12.5, 4.0))):
         ts(r("pio", k, k + 1), own, a, O.is_gt, b, O.mult)
-    for k in range(3):
-        tt(r("pio", 3, 4), r("pio", k, k + 1), r("pio", 3, 4) if k else own, O.add)
+    zero(r("ct", 512, 768), r("onet", 0, 256))
     for k in range(4):
         if k % 2:
             lin(r("ubt", k, 512, 4), r("ones"), 0.0, r("ut", k, k + 1))
         else:
             ts(r("ubt", k, 512, 4), r("onet", 0, 128), r("ut", k, k + 1), O.mult)
-    zero(r("ct", 512, 768), r("onet", 0, 256))
+    lin(r("cn", 16, 17), r("paf", 2, 3), 16.0, 0.0)
+    lin(r("cn", 17, 18), r("paf", 2, 3), 16.0, 64.0)
     lin(r("t16", 0, 192, 16), r("ones", 0, 12), 0.0, -1000.0)
     lin(r("cn", 1, 2), own, 1.0, 0.5)
-    lin(corr, own, 32.0, -480.0, F.Square)
     lin(r("cn", 10, 11), r("paf", 0, 1), -4.0, 256.0)
     lin(r("cn", 11, 12), r("paf", 0, 1), 4.0, 0.0)
-    zero(r("eht"), r("onet"))
+    for k in range(2):
+        lin(r("wct", 512 + k, 1024, 2), r("onet", 0, 256), 0.0, r("cn", 16 + k, 17 + k))
     qz("uq", 0, 128, r("ubt"))
 
     qz("tq", 0, 192, r("tbt"))
@@ -305,12 +312,22 @@ def rank_program(g, core, T, topo):
     mm(1, "tq", 0, "uq", 0, 128)
     mm(2, "tq", 64, "uq", 0, 128)
     mm(6, "uq", 0, "tq", 0, 192)
-    ts(r("dq"), r("t16"), r("cn", 1, 2), O.subtract, STEP, O.mult)
+    ts(r("wct", 0, 512), r("onet", 0, 512), own, O.mult)
     move("lb", K, "tq", K, 80, "dpad", 32)
 
     lin(r("sg"), r("ps6", 0, 192), 1.0, 0.0, F.Sign)
+    zero(r("vn", 0, 512), r("onet", 0, 512))
     issue("a", [r("sg")], [r("sg1"), r("msgf", 0, 1)], lambda: A.activation(
         ap(r("sg1")), ap(r("sg")), F.Relu, accum_out=ap(r("msgf", 0, 1))))
+    lin(corr, own, 32.0, -480.0, F.Square)
+    zero(r("vn", 512, 768), r("onet", 0, 256))
+    zero(r("eht"), r("onet"))
+    lin(r("nr8", *six), r("ir", *six), -0.125, 0.0)
+    lin(r("key"), r("ones", 0, 16), 0.0, -100.0)
+    lin(r("nc8", *six), r("ir", *six), -0.125, corr)
+    lin(r("cn", 14, 15), own, 1.0, -6.0, F.Relu)
+    lin(r("cn", 5, 6), own, 32.0, -32.0 * (sh + 5), F.Square)
+    lin(r("nw", 0, 3), r("m16", 0, 3), 1.0, own)
 
     def lower(src, a=0, b=192):
         return r(src, a, b, 1, 64, 128)
@@ -329,12 +346,8 @@ def rank_program(g, core, T, topo):
     def tie1(sp1):
         ts(r("ct", 515, 768, 4, 64), r("sm1", 0, 64, 1, 64), sp1, O.is_equal)
 
-    def rank_ops():
-        qz("cq", 0, 192, r("ct"))
-        mm(3, "oneq", 0, "cq", 0, 192)
-
-    def order_ops(out, a, b):
-        return [lambda: select(r("sc2", a, b), r("prm", a, b), a, b),
+    def order_ops(out, a, b, src):
+        return [lambda: select(r("sc2", a, b), src, a, b),
                 lambda: ts(out, r("sc2", a + 15, b, 16), corr, O.subtract)]
 
     s0, s1 = r("ps1", 0, 1), r("ps2", 0, 1, 1, 64)
@@ -342,52 +355,66 @@ def rank_program(g, core, T, topo):
     tt(r("sm"), r("ps0", 0, 128), r("bm"), O.add)
     low1("ps0")
     gts[0]()
-    tie0(s0)
     gts[1]()
+    tie0(s0)
     gts[2]()
     tie1(s1)
-    rank_ops()
+    qz("cq", 0, 192, r("ct"))
     mm(4, "cq", 0, "oneq", 0, 128)
     mm(5, "cq", 64, "oneq", 0, 128)
-    ts(r("idt"), r("ipd"), 0.0, O.is_equal, 0.5, O.mult)
-    ac(r("eht", 3, 515, 4), r("idt"))
+    qz("oneq", 128, 256, r("wct"))
+
+    def hot(a, b):
+        ts(r("vn", 4 * a, 4 * b, 4), r("irb", a, b), r("ps4", 0, 1), O.is_equal)
+        ts(r("vn", 4 * a + 1, 4 * b, 4, 64), r("irb", a, b, 1, 64), r("ps5", 0, 1, 1, 64), O.is_equal)
+
+    def order(k, a):
+        qz("cq", a, 128, r("vn", 4 * a, 4 * a + 512))
+        mm(k, "oneq", 128, "cq", a, 128, True, False)
+        mm(k, "oneq", 256, "cq", a, 128, False, True)
 
     my_land = r("land", 8 * me, 8 * me + 1)
-    select(r("sc"), r("ps3", 0, 192), 0, 192)
     ts(r("msgf", 1, 2), r("msgf", 0, 1), r("cn", 10, 11), O.mult, r("ps4", 0, 1), O.add)
-    ts(r("rof"), r("sc", 15, 192, 16), corr, O.subtract)
+    hot(0, 128)
     ts(my_land, r("ps5", 0, 1), r("cn", 11, 12), O.mult, r("msgf", 1, 2), O.add)
     spread(my_land, my_land, "am")
-    scatter(r("prm"), r("ir", 0, 192), r("rof"))
-    weave(order_ops(r("ol", 0, 3), 0, 48))
+    order(3, 0)
+    ts(r("dq"), r("t16"), r("cn", 1, 2), O.subtract, STEP, O.mult)
+    hot(128, 192)
+    low = order_ops(r("ol", 0, 3), 0, 48, r("ps3", 0, 48))
+    low[0]()
+    ts(r("idt"), r("ipd"), 0.0, O.is_equal, 0.5, O.mult)
+    low[1]()
+    ts(r("cn", 12, 13), own, sh + 5.5, O.is_gt, 0.5, O.mult)
+    ts(r("cn", 13, 14), own, sh - 0.5, O.is_lt, 0.5, O.mult)
     pick("ls", 0, 48, "tq", 0, 192, r("ol", 0, 3), [(0, 192)])
     for x, y in zip(both("ls", 0, K), both("w0", K * me, K * me + K)):
         spread(x, y, "al")
     move("w0", K * me, "ls", 0, K, "dls")
 
-    six = (0, 6)
-    lin(r("nr8", *six), r("ir", *six), -0.125, 0.0)
-    lin(r("key"), r("ones", 0, 16), 0.0, -100.0)
-    lin(r("cn", 2, 3), own, 1.0, -6.0, F.Relu)
-    lin(r("nw", 0, 3), r("m16", 0, 3), 1.0, own)
+    order(2, 64)
+    ac(r("eht", 3, 515, 4), r("idt"))
+    lin(r("cn", 15, 16), r("cn", 12, 13), 1.0, r("cn", 13, 14))
+    lin(r("cn", 14, 15), r("cn", 14, 15), 1.0, 2.5)
+    lin(r("cn", 3, 4), r("cn", 5, 6), 1.0, corr)
     lin(r("nws", 0, 3), r("nw", 0, 3), 1.0 / K, 0.0)
-    weave([lambda: fill(r("fb"), 0)], order_ops(r("om", 0, 3), 48, 96),
-          [idle, lambda: qz("nq", 0, 176, r("nzt"))])
-    pick("nb", 0, 48, "tq", 0, 192, r("om", 0, 3), [(0, 192)])
+    lin(r("cn", 2, 3), r("cn", 14, 15), 1.0, r("cn", 15, 16))
     lin(r("cn", 4, 5), own, 6.0, 0.0)
-    lin(r("v1r"), r("rke"), 16.0, r("pio", 3, 4))
     lin(r("cn", 6, 7), corr, 1.0, float(K))
     lin(r("cn", 7, 8), r("ones", 0, 1), 0.0, 0.5 - K)
     lin(r("cn", 8, 9), r("ones", 0, 1), 0.0, 0.5 - 2 * K)
+    weave([lambda: fill(r("fb"), 0)], order_ops(r("om", 0, 3), 48, 96, r("ps3", 48, 96)),
+          [lambda k=k: tt(r("pio", 3, 4), r("pio", k, k + 1), r("pio", 3, 4) if k else own, O.add) for k in range(3)],
+          [lambda: qz("nq", 0, 176, r("nzt"))], order_ops(r("ol", 6, 12), 96, 192, r("ps2", 32, 128)))
+    pick("nb", 0, 48, "tq", 0, 192, r("om", 0, 3), [(0, 192)])
+    pick("hp", 0, TH, "tq", 0, 192, r("ol", 6, 12), [(0, 192)])
+    lin(r("hq", mate + sh, mate + sh + 1), r("ones", 0, 1), 0.0, float(HX + TH * 3 - 2 * K))
+    lin(r("v1r"), r("rke"), 16.0, r("pio", 3, 4))
     lin(r("cn", 9, 10), r("pio", 3, 4), 1.0, 16.0 * me)
-    zero(r("hq"), r("ones", 0, 16))
-    for x in range(N):
-        lin(r("hq", x + sh, x + sh + 1), r("ones", 0, 1), 0.0, float(HX + TH * (3 if x == mate else third(x)) - 2 * K))
+    lin(r("rsq"), r("x48", 0, 32), 0.0, 1.0)
     lin(r("cnx"), r("cnx"), 1.0, own)
     lin(r("rho", 84, 96), r("ones", 0, 12), 0.0, 0.0)
-    lin(r("rsq"), r("x48", 0, 32), 0.0, 1.0)
     lin(r("rsq", 0, 32, 16), r("ones", 0, 2), 0.0, 0.0)
-    lin(r("sw", HX, NX + 8), r("ir", 0, 392), 0.0, BIG)
 
     def unit(k):
         qz("eq", 128 * k, 128, r("eht", 3 - k, 515 - k))
@@ -396,16 +423,15 @@ def rank_program(g, core, T, topo):
         for k in range(4):
             mm(4 + k, "eq", 128 * k, "nq", K * t, 128, True, stop)
 
-    def places(k, val, zr):
+    def places(k, ref, val, zr):
         pu, tpu = r("pt", 4 * k, 4 * k + 1), r("pt", 4 * k + 2, 4 * k + 3)
         pl, t5 = r("pl", k, k + 1), r("t5", k, k + 1)
-        select(r("ks"), r("key"), 0, 16)
-        ts(r("gt", *six), r("key", *e6), corr, O.add, r("ks", 15, 16), O.is_gt)
-        issue("v", [r("gt", *six)], [pl], lambda: V.tensor_reduce(ap(pl), ap(r("gt", *six)), AxisListType.X, O.add))
-        ts(pu, pl, r("cn", 2, 3), O.add)
-        ts(t5, pl, -1.0, O.mult, 5.0, O.add)
+        issue("a", [r("k2", *six), ref], [r("gt", *six), pl], lambda: A.activation(
+            ap(r("gt", *six)), ap(r("k2", *six)), F.Sign, bias=ap(ref), scale=-1.0, accum_out=ap(pl)))
+        ts(pu, pl, -0.5, O.mult, r("cn", 2, 3), O.add)
+        ts(t5, pl, -1.0, O.mult, pl, O.max)
         scatter(r("wr%d" % k), val, pu)
-        ts(tpu, t5, pl, O.min)
+        ts(tpu, t5, -0.5, O.mult, 2.5, O.add)
         if k:
             scatter(r("wb"), r("b32"), pu)
         gather(zr, r("wr%d" % k), tpu)
@@ -428,15 +454,19 @@ def rank_program(g, core, T, topo):
     unit(2)
     cp(r("l6"), r("ir", *six))
     ts(r("ia"), r("ipd", 0, 32), 15, O.bitwise_and)
-    ts(r("dm"), r("ia"), 0.0, O.is_equal)
     ts(r("hi", *six), r("land", 0, 48, 8), 1.0 / 256, O.mult, -127.5 / 256, O.add)
     issue("g", [r("hi", *six)], [r("fb", *e6)], lambda: g.partition_broadcast(
         ap(r("fb", *e6)), ap(r("hi", 0, 6, 1, 0, 1)), 128))
     cp(r("v6", *six), r("land", 0, 48, 8))
     unit(3)
     noise(0, False)
+    ts(r("dm"), r("ia"), 0.0, O.is_equal)
     tt(r("key", *e6), r("fb", *e6), r("nr8", *six), O.add)
-    pu, tpu = places(0, r("rke"), r("zr0"))
+    tt(r("k2", *six), r("fb", *e6), r("nc8", *six), O.add)
+    select(r("ks"), r("key"), 0, 16)
+    qz("wq", 0, 256, r("wt"))
+    pu, tpu = places(0, r("ks", 15, 16), r("rke"), r("zr0"))
+    scatter(r("wf"), r("fb"), pu)
     ts(r("oll", 0, 3), r("nws", 0, 3), r("zr0", em, em + 1), O.add, float(K), O.mult)
     cp(r("rw", 48, 54), r("v6", *six))
 
@@ -445,14 +475,14 @@ def rank_program(g, core, T, topo):
     for k in range(8):
         dma("s", r("rw", 0, 48, 1, 16 * k, 16 * k + 16), ("mdr", 0, 16, 0, 48, 1), "drw", 128)
 
-    note(0, 1.0)
     ts(r("tk", 0, 1), r("zr0", em, em + 1), float(me), O.not_equal, 64.0, O.mult)
-    scatter(r("wf"), r("fb"), pu)
-    ts(r("ox", 0, 3), r("nw", 0, 3), r("tk", 0, 1), O.add)
     anew("lb", r("oll", 0, 3), [(0, 288)], 288)
+    note(0, 1.0)
+    ts(r("ox", 0, 3), r("nw", 0, 3), r("tk", 0, 1), O.add)
     gather(r("fa"), r("wf"), tpu)
     scatter(r("wc"), r("hq"), pu)
     tt(r("t0", *six), r("zr0", *e6), r("ir", *six), O.not_equal)
+    ts(r("ob"), r("zr0", *e6), r("cn", 4, 5), O.add)
     gather(r("cz"), r("wc"), tpu)
     weave(pack_ops("nb", 64))
     pick("xs", 0, 48, "nb", 0, 192, r("ox", 0, 3), [(0, 48), (64, 192)])
@@ -460,16 +490,7 @@ def rank_program(g, core, T, topo):
         spread(x, y, "ax", "an")
     move("w0", LX + K * me, "xs", 0, K, "dxs")
     noise(1, True)
-    for k in range(4):
-        ac(r("dn", K * k, K * k + K), r("ps%d" % (4 + k), 0, K))
-    weave(order_ops(r("ol", 6, 12), 96, 192), [lambda: ts(r("ob"), r("zr0", *e6), r("cn", 4, 5), O.add)])
-    pick("hp", 0, TH, "tq", 0, 192, r("ol", 6, 12), [(0, 192)])
-    for x, y in zip(both("hp", 0, TH), both("hp", TH, 2 * TH)):
-        send([([mate], out_eng, x, y, "ah")], x)
-    move("w0", HX + TH * third(me), "hp", 0, TH, "dhb", 64)
-    move("w0", HX + TH * 3, "hp", TH, TH, "dhb", 64)
     mm(1, "uq", 0, "w0", 0, 288)
-    qz("wq", 0, 256, r("wt"))
 
     fit = [
         lambda: lin(r("r96", *six), r("fa", *e6), 1.0, float(K - P + K), F.Relu),
@@ -479,7 +500,9 @@ def rank_program(g, core, T, topo):
         lambda: tt(r("v1", *six), r("u1", *six), r("r144", *six), O.subtract),
         lambda: tt(r("fan", *six), r("fan", *six), r("u1", *six), O.subtract),
         lambda: tt(r("v1", *six), r("v1", *six), r("t0", *six), O.mult),
-        lambda: tt(r("apre", *six), r("fan", *six), r("v1", *six), O.add)]
+        lambda: tt(r("key", *e6), r("fan", *six), r("v1", *six), O.add),
+        lambda: select(r("ks"), r("key"), 0, 16),
+        lambda: ts(r("ap3", *six), r("key", *e6), r("ks", 15, 16), O.subtract, r("cn", 3, 4), O.add)]
     bases = [
         lambda: lin(r("c1", *six), r("t0", *six), float(LX), 0.0),
         lambda: lin(r("bz", *six), r("zr0", *e6), float(K), float(LX - K)),
@@ -490,9 +513,7 @@ def rank_program(g, core, T, topo):
         lambda: gather_a(r("hc"), r("hc2"), r("l6"), 0.5),
         lambda: gather_a(r("hb"), r("hb2"), r("l6"), 0.5),
         lambda: gather_a(r("ca"), r("cb"), r("l6"), 0.5),
-        lambda: ts(r("bzf"), r("zr0"), *((min(far) - 0.5, O.is_gt) if me < min(far) else (max(far) + 0.5, O.is_lt)), TH, O.mult),
-        lambda: lin(r("b32"), r("bzf"), 1.0, own),
-        lambda: ac(r("sw", 0, 288), r("ps1", 0, 288))]
+        lambda: ts(r("bzf"), r("zr0"), *((min(far) - 0.5, O.is_gt) if me < min(far) else (max(far) + 0.5, O.is_lt)), TH, O.mult)]
     where = [
         lambda: ts(r("hw"), r("rw"), 1.0 / 256, O.mult, -127.5 / 256, O.add),
         lambda: cp(r("vf"), r("rw")),
@@ -503,12 +524,23 @@ def rank_program(g, core, T, topo):
         lambda: tt(r("yt"), r("rho"), r("ca"), O.add, r("ob")),
         lambda: lin(r("sb"), r("rg"), 1.0, r("cn", 7, 8), F.Sign),
         lambda: lin(r("sd"), r("rg"), 1.0, r("cn", 8, 9), F.Sign),
+        lambda: lin(r("b32"), r("bzf"), 1.0, own),
+        lambda: ac(r("sw", 0, 288), r("ps1", 0, 288)),
         lambda: tt(r("sb"), r("sb"), r("hb"), O.mult),
         lambda: tt(r("sd"), r("sd"), r("hc"), O.mult),
         lambda: tt(r("yt"), r("yt"), r("sb"), O.add),
         lambda: tt(r("y0g"), r("yt"), r("sd"), O.add)]
-    weave(bases, fit)
-    weave(where)
+    weave(bases, fit, [idle] * 5 + where[:5])
+    for q in ("g", "s"):
+        before(q, [r("hc2", *six)], [])
+    for x, y in zip(both("hp", 0, TH), both("hp", TH, 2 * TH)):
+        send([([mate], out_eng, x, y, "ah")], x)
+    move("w0", HX + TH * third(me), "hp", 0, TH, "dhb", 64)
+    move("w0", HX + TH * 3, "hp", TH, TH, "dhb", 64)
+    weave(where[5:])
+    lin(r("sw", HX, NX + 8), r("onet", 0, 392), 0.0, BIG)
+    for k in range(4):
+        ac(r("dn", K * k, K * k + K), r("ps%d" % (4 + k), 0, K))
 
     chip = min([me] + near)
     for k, a in ((0, K * chip), (2, K * min(far))):
@@ -516,8 +548,9 @@ def rank_program(g, core, T, topo):
         ts(r("pos", a, a + 144), r("ps%d" % k, 0, 144), 0.0, O.is_gt)
         ac(r("sw", LX + a, LX + a + 144), r("ps%d" % k, 0, 144))
         scan(r("psc", a, a + 144), r("x48", a, a + 144), r("pos", a, a + 144))
-    tt(r("key", *e6), r("psc", 47, 288, 48), r("apre", *six), O.add)
-    pu, tpu = places(1, r("v1r"), r("zg"))
+    scan(r("ks", *six), r("dq", *e6), r("psc", 47, 288, 48), O.add, O.max)
+    tt(r("k2", *six), r("psc", 47, 288, 48), r("ap3", *six), O.add)
+    pu, tpu = places(1, r("ks", 5, 6), r("v1r"), r("zg"))
     og, ofs = r("zg", em, em + 1), r("osl", 0, 12)
     gather(r("bzf"), r("wb"), tpu)
     gather(r("osl"), r("y0g"), og)
@@ -526,10 +559,10 @@ def rank_program(g, core, T, topo):
         x = near[i] + sh
         ts(r("oh", 6 * i, 6 * i + 6), r("n6"), r("bzf", x, x + 1), O.add)
     holder(0)
+    holder(1)
     tt(r("m32"), r("sw"), r("dm"), O.mult, r("osl", 12, 14))
     gather_a(r("st"), r("sw"), ofs)
-    gather_a(r("l16"), r("y0g"), og)
-    holder(1)
+    tt(r("sm"), r("sw"), r("bm"), O.add, r("osl", 0, 8))
     scan(r("sq"), r("rsq"), r("m32"), O.mult)
     s0, s1 = r("sq", 15, 16), r("sq", 31, 32, 1, 64)
 
@@ -538,8 +571,8 @@ def rank_program(g, core, T, topo):
         send([([z], all_eng[h_all * i:h_all * i + h_all], r(x, TH * i, TH * i + TH), y, "a3") for i, z in enumerate(near)],
              r(x))
 
-    tt(r("sm"), r("st", 0, 128), r("bm"), O.add)
     lin(r("sgn", 0, 192, 1, 64), lower("st"), -1.0, s1, F.Sign)
+    gather_a(r("l16"), r("y0g"), og)
     lin(r("ct", 1, 768, 4, 64), r("sgn", 0, 192, 1, 64), -1.0, 0.0, F.Relu)
     gts = gt_ops("st", s0, s1)
     low1("st")
@@ -548,7 +581,8 @@ def rank_program(g, core, T, topo):
     gts[1]()
     tie1(s1)
     ts(r("ofz"), ofs, float(HX - 1), O.min)
-    rank_ops()
+    qz("cq", 0, 192, r("ct"))
+    mm(3, "oneq", 0, "cq", 0, 192)
 
     pick("tz", 0, 192, "w0", 0, 576, r("ofz"), [(0, 576)])
     note(1, 1.0 / 16)
@@ -557,10 +591,9 @@ def rank_program(g, core, T, topo):
     for k in range(2):
         ac(r("d%d" % k), r("ps%d" % (4 + k), 0, 192))
     select(r("sc"), r("ps3", 0, 192), 0, 192)
-    ts(r("tk", 0, 1), r("zg", em, em + 1), r("cn", 9, 10), O.not_equal)
+    ts(r("tk", 0, 1), r("zg", em, em + 1), r("cn", 9, 10), O.not_equal, r("cn", 6, 7), O.mult)
     ts(r("roc"), r("sc", 15, 192, 16), corr, O.subtract, K - 1.0, O.min)
-    tt(r("dlt", 0, 12), r("cnx"), r("l16", 0, 12), O.subtract)
-    ts(r("fm", 0, 12), r("sc", 15, 192, 16), r("cn", 6, 7), O.is_lt, r("tk", 0, 1), O.mult)
+    ts(r("fm", 0, 12), r("sc", 15, 192, 16), r("tk", 0, 1), O.is_lt)
     for k in (2, 3):
         gather_a(r("g%d" % k), r("dn", K * k, K * k + K), r("roc"))
 
@@ -570,25 +603,28 @@ def rank_program(g, core, T, topo):
         else:
             tt(r("vn", k, 768, 4), r("ps%d" % (4 + k), 0, 192), r("g%d" % k), O.add)
     make(0)
-    tt(r("fl", 0, 12), r("fm", 0, 12), r("dlt", 0, 12), O.mult)
+    tt(r("fl", 0, 12), r("fm", 0, 12), r("cnx"), O.mult)
     make(1)
-    tt(r("fl", 0, 12), r("fl", 0, 12), r("l16", 0, 12), O.add)
+    tt(r("fl", 0, 12), r("fl", 0, 12), r("l16", 0, 12), O.max)
     make(2)
     make(3)
     cp(r("ofin"), r("fl", 0, 12))
     qz("w0", NX, 192, r("vn"))
-    pick("fin", 0, 192, "w0", 0, 1152, r("ofin"), [(0, 1152)])
+    pick("fin", 0, 128, "w0", 0, 1152, r("ofin", 0, 8), [(0, 1152)])
+    pick("fin", 128, 64, "w0", 0, 1152, r("ofin", 8, 12), [(0, 1152)])
 
-    dma("s", T.oc[:, :], r("fin"), "dout", 128)
-    mm(1, "wq", 0, "fin", 0, 192)
+    mm(1, "wq", 0, "fin", 0, 128)
     mm(2, "wq", 128, "fin", 0, 128)
     mm(3, "wq", 128, "fin", 64, 128)
+    mm(0, "wq", 0, "fin", 64, 128)
+    dma("s", T.oc[:, :], r("fin"), "dout", 128)
     for k in range(4):
-        dma("s" if k < 2 else "a", T.osc[4 * k:4 * k + 4, :], r("fin_s", 0, 192, 1, 32 * k, 32 * k + 4), "dout", 128)
-    cp(r("ysb", 0, 192), r("ps1", 0, 192))
-    dma("s", T.y[:, 0:192], r("ysb", 0, 192), "dout", 128)
+        dma("s" if k < 3 else "a", T.osc[4 * k:4 * k + 4, :], r("fin_s", 0, 192, 1, 32 * k, 32 * k + 4), "dout", 128)
+    cp(r("ysb", 0, 128), r("ps1", 0, 128))
     ac(r("ysb", 192, 320), r("ps2", 0, 128))
-    cp(r("ysb", 320, 384), r("ps3", 64, 128))
+    ac(r("ysb", 320, 384), r("ps3", 64, 128))
+    cp(r("ysb", 128, 192), r("ps0", 64, 128))
+    dma("s", T.y[:, 0:192], r("ysb", 0, 192), "dout", 128)
     dma("a", T.y[:, 192:384], r("ysb", 192, 384), "dout", 128)
     dma("s", T.od[:, :], r("odt", 0, 12, 1, 0, 1), "dout", 128)
 

@@ -2,43 +2,43 @@ from concourse.bass import DstId, RemoteDMATransfer
 from concourse.mybir import dt, AluOpType as O, ActivationFunctionType as F
 
 P, K, N = 192, 48, 6
-LX, HX, NX = 288, 576, 960
+LX, PAD, HX, NX = 288, 576, 592, 976
 TH = 96
 BIG = 1e29
 STEP = 2048.0
 
-SCRATCH = {"mdr": ("dram", [16, 48], "uint16")}
+SCRATCH = {}
 ARENA = {}
 for _d, _l in (
-        ("bfloat16", "ut 4 tbt 768 nzt 704 wt 1024 ubt 512 onet 516 eht 516 vt 512 vn 768 ct 768 idt 128 x48 288 pos 288 psc 288 "
-                     "wct 1024 irb 192"),
-        ("int32", "ipd 128 pi 2 pa 6 ia 32 hi 8 fb 16 hw 54"),
-        ("float32", "ir 8 m16 4 t16 192 dq 192 ones 128 paf 6 cn 24 bm 128 dm 32 nw 4 nws 4 nr8 8 "
+        ("bfloat16", "ut 4 tbt 768 nzt 704 wt 1024 ubt 512 half 516 eht 516 vt 512 vn 768 ct 768 x48 288 pos 288 psc 288 "
+                     "wct 512 irb 384"),
+        ("int32", "pi 4 pa 6 hi 8 fb 16"),
+        ("float32", "ipd 128 i16 32 ir 8 m16 4 t16 192 dq 192 ones 32 paf 6 pf 2 cn 24 bm 128 dm 32 nw 4 nws 4 nr8 8 "
                     "rsq 32 c48 8 sm 128 sm1 64 sg 192 sg1 192 sc 192 sc2 192 "
-                    "msgf 2 sw 968 dn 192 d0 192 d1 192 g2 192 g3 192 v1r 16 rke 16 cnx 12 n6 6 bzf 16 sgn 192 "
-                    "st 192 m32 32 sq 32 ysb 384 odt 16 rho 96 hq 16 ca 96 hb 96 hc 96 sb 96 sd 96 rg 96 pio 4"),
-        ("uint16", "land 48 v6 8 rw 54 l6 6 ol 12 oll 4 om 4 ox 4 ob 6 zg 16 osl 16 oh 12 ofz 12 roc 12 ofin 12 pt 8")):
+                    "msgf 2 sw 592 dn 192 d0 192 g1 192 d2 192 g3 192 v1r 16 rke 16 cnx 12 n16 96 y1g 96 bzf 8 sgn 192 "
+                    "st 192 m32 32 sq 32 ysb 384 odt 16 rho 136 tm 64 t1 64 t2 128 dl 8 hq 16 ca 96 hb 96 hc 96 sb 96 sd 96 "
+                    "rg 96"),
+        ("uint16", "land 48 odl 8 l6 6 ol 12 oll 4 om 4 ox 4 ob 6 zg 16 osl 16 oh 64 roc 12 ofin 12 pt 8")):
     _w = _l.split()
     for _k, _n in zip(_w[::2], _w[1::2]):
         SCRATCH[_k] = ("sbuf", [128, int(_n)], _d)
-_w = ("tq 192 nq 176 wq 256 uq 128 oneq 384 eq 512 cq 192 ls 48 nb 192 hp 192 hs 192 lb 128 tz 192 xs 48 w0 1152 "
-      "fin 192").split()
+_w = "tq 192 nq 176 wq 256 uq 128 oneq 256 eq 512 cq 192 nb 192 hp 192 hr 96 hs 192 lb 128 tz 192 w0 1168 fin 192".split()
 for _k, _n in zip(_w[::2], _w[1::2]):
     SCRATCH[_k] = ("sbuf", [128, int(_n)], "float8_e4m3fn_x4")
     SCRATCH[_k + "_s"] = ("sbuf", [128, int(_n)], "uint8")
 for _k in range(8):
     SCRATCH["ps%d" % _k] = ("psum", [128, 512], "float32")
 _o = 0
-for _n, _l in ((54, "vf h2"), (96, "y0g yt"),
-               (16, "key ks zr0 zr1 wr0 wr1 wf wb wc cz fa b32 l16 fl fm"),
-               (8, "gt pl t5 t0 k2 nc8 ap3 fan r96 r144 u1 v1 c1 bz cb hb2 hc2 tk")):
+for _n, _l in ((96, "y0g yt yc"),
+               (16, "key ks zr0 zr1 wr0 wr1 wf wc cz fa l16 fl fm"),
+               (8, "gt pl t5 t0 k2 nc8 ap3 fan r96 r144 u1 v1 c1 bz cb hb2 hc2 tk vf h2 hf")):
     for _k in _l.split():
         ARENA[_k] = (_o, _n)
         _o += _n + (-_n) % 8
 SCRATCH["ar"] = ("sbuf", [128, _o], "float32")
 
-DMAS = ["du", "dtb", "dnz", "dw", "dpv", "dpad", "dls", "dhb", "dmd", "drw", "dxs", "dout"]
-SEMAPHORES = ["cv", "ca", "ct", "cg", "am", "al", "ah", "ax", "an", "a3", "left"] + DMAS
+DMAS = ["du", "dtb", "dnz", "dw", "dpv", "dpad", "dhb", "dout", "dct", "dvn"]
+SEMAPHORES = ["cv", "ca", "ct", "cg", "am", "al", "ah", "ax", "an", "a3", "left", "r0", "r1"] + DMAS
 
 
 def r(name, a=0, b=None, step=1, p=0, q=128):
@@ -55,16 +55,82 @@ def covers(x, y):
     return x[1] <= y[1] and y[2] <= x[2] and x[3] <= y[3] and y[4] <= x[4] and (x[5] == 1 or x[5] == y[5] and x[3] == y[3])
 
 
-def weave(*chains):
-    for k in range(max(len(c) for c in chains)):
-        for c in chains:
-            if k < len(c):
-                c[k]()
+WAKE = 0.16
+ORDER = [int(_k) for _k in """
+33 0 52 50 10 11 12 13 15 14 34 16 17 1 2 3 4 5 6 7 8 9 36 37 49 39 51 78 54 42 38 47 43 40 46 44 58 48 45 53 79 81 80 82 83 84
+88 87 91 93 90 92 89 94 71 76 85 86 68 55 60 95 96 97 101 98 102 103 113 114 104 99 100 105 75 106 115 107 121 77 108 57 56 59
+122 63 62 67 61 134 116 109 111 24 25 19 26 110 112 119 117 120 73 123 74 118 72 135 136 148 137 138 139 150 149 151 124 130 140
+158 157 132 133 131 125 127 18 21 23 27 30 31 32 22 28 20 35 126 128 141 142 143 144 152 145 70 147 191 165 192 195 171 69 129
+155 154 166 156 153 208 230 207 197 198 169 167 170 168 159 172 175 160 176 174 161 173 146 188 189 186 187 190 177 41 178 162
+163 200 196 209 201 199 193 211 203 194 202 216 210 204 212 205 179 65 64 164 231 233 232 218 234 221 220 214 213 215 222 66 180
+183 29 181 182 184 185 217 224 219 235 239 228 229 236 223 238 225 240 206 242 244 243 226 237 241 245 247 246 249 248 227
+250 254 255 256 258 259 252 257 268 270 279 261 263 253 269 251 307 271 272 273 274 275 260 276 278 262 277 280 282 281 283 264
+266 265 267 284 286 285 295 287 291 289 293 288 296 292 290 294 297 298 299 301 300 302 312 303 306 304 305 309 311 310 308 313
+316 315 314 318 317
+""".split() if _k.isdigit()]
+PLAN = {}
+
+
+def plan(ops):
+    n = len(ops)
+    pre = [dict() for _ in range(n)]
+    seen = {}
+    for j, (q, rs, ws, _, _, after) in enumerate(ops):
+        for i in after:
+            pre[j][i] = 0.0
+        for x, w in [(x, False) for x in rs] + [(x, True) for x in ws]:
+            bank = SCRATCH[x[0]][0] == "psum"
+            for i, y, v in seen.get(x[0], ()):
+                if i != j and not q == "x" == ops[i][0] and ((w or v) and meet(x, y) or bank and ops[i][0] != q):
+                    pre[j][i] = 0.0 if q == "t" == ops[i][0] else WAKE
+        for x, w in [(x, False) for x in rs] + [(x, True) for x in ws]:
+            seen.setdefault(x[0], []).append((j, x, w))
+    PLAN["ops"], PLAN["pre"] = ops, pre
+    where = {j: k for k, j in enumerate(ORDER)}
+    if len(where) == n and all(where[i] < where[j] for j in range(n) for i in pre[j]):
+        return ORDER
+    PLAN["bad"] = True
+    return list(range(n))
 
 
 def rank_program(g, core, T, topo):
+    def far_of(x):
+        return [y for y in range(N) if topo.chip(T.cores[y]) != topo.chip(T.cores[x])]
+
+    def near_of(x):
+        return [y for y in range(N) if y != x and y not in far_of(x)]
+
+    def third(x):
+        return [y for y in range(N) if y not in far_of(x)].index(x)
+
+    def mate_of(x):
+        return [y for y in far_of(x) if third(y) == third(x)][0]
+
+    def helper(x):
+        c = T.cores[x]
+        here = [y for y in [x] + near_of(x) if topo.die(T.cores[y]) == topo.die(c)]
+        if 2 * len(here) <= len(near_of(x)) + 1:
+            return None
+        free = [d for d in topo.cores_of(c) if topo.die(d) != topo.die(c) and T.rank_of(d) is None
+                and topo.may_write(d, T.cores[mate_of(x)])]
+        return free[sorted(here).index(x)]
+
+    def address(c):
+        a = topo.addr(c)
+        return DstId(rid=a[0], pnc=a[1])
+
     me = T.rank_of(core)
     if me is None:
+        for x in range(N):
+            if helper(x) == core:
+                to = T.cores[mate_of(x)]
+                n_in = len(topo.engines(T.cores[x], core)) - len(topo.engines(T.cores[x], to))
+                for sem, a, b in (("r0", T["hr"][:, 0:TH].bitcast(dt.uint8), T["hp"][:, TH:2 * TH].bitcast(dt.uint8)),
+                                  ("r1", T["hr_s"][:, 0:TH], T["hp_s"][:, TH:2 * TH])):
+                    g.wait_ge(T.sem[sem], n_in)
+                    g.remote_dma_fused([RemoteDMATransfer(dst_ids=[address(to)], dma_engine_mask=topo.mask(core, to),
+                                                          remote_sem=T.sem["ah"], srcs=[a], dsts=[b])], local_sem=T.sem["left"])
+                g.wait_ge(T.sem["left"], 2 * len(topo.engines(core, to)))
         return
     queue = {"v": g.vector, "a": g.scalar, "t": g.tensor, "g": g, "s": g.sync}
     V, A, X = g.vector, g.scalar, g.tensor
@@ -100,7 +166,21 @@ def rank_program(g, core, T, topo):
             d[x[0]] = [e for e in d.get(x[0], ()) if not covers(x, e[0])]
         wr[x[0]].append((x, tok))
 
-    def issue(q, reads, writes, fn, sem=None, total=0, adds=False):
+    ops, calls = [], []
+
+    def width(x):
+        return (x[4] - x[3] + x[5] - 1) // x[5]
+
+    def narrow(*xs):
+        return 0.5 if all(SCRATCH[x[0]][2] in ("bfloat16", "uint16") for x in xs) else 1.0
+
+    def issue(q, reads, writes, fn, sem=None, total=0, adds=False, time=None, per=1.0):
+        if time is None:
+            time = {"v": 0.04, "a": 0.08}[q] + max(0.053, 0.00083 * per * width(writes[0]))
+        ops.append((q, reads, writes, 0.05 if sem else time, time, []))
+        calls.append(lambda: emit(q, reads, writes, fn, sem, total, adds))
+
+    def emit(q, reads, writes, fn, sem, total, adds):
         before(q, reads, writes, adds)
         if sem is None:
             count[q] += 1
@@ -129,18 +209,23 @@ def rank_program(g, core, T, topo):
     def ts(out, in0, s1, op0, s2=None, op1=None):
         rs = [in0] + [s for s in (s1, s2) if isinstance(s, tuple)]
         if op1 is None:
-            issue("v", rs, [out], lambda: V.tensor_scalar(ap(out), ap(in0), num(s1), None, op0))
+            issue("v", rs, [out], lambda: V.tensor_scalar(ap(out), ap(in0), num(s1), None, op0), per=narrow(out, in0))
         else:
-            issue("v", rs, [out], lambda: V.tensor_scalar(ap(out), ap(in0), num(s1), num(s2), op0, op1))
+            issue("v", rs, [out], lambda: V.tensor_scalar(ap(out), ap(in0), num(s1), num(s2), op0, op1), per=narrow(out, in0))
 
     def tt(out, a, b, op, off=None):
         if off is None:
-            issue("v", [a, b], [out], lambda: V.tensor_tensor(ap(out), ap(a), ap(b), op))
+            issue("v", [a, b], [out], lambda: V.tensor_tensor(ap(out), ap(a), ap(b), op),
+                  per=1 if "psum" in (SCRATCH[a[0]][0], SCRATCH[b[0]][0]) else 2)
         else:
-            issue("v", [a, b, off], [out], lambda: V.tensor_tensor(ap(out), ap(a).indirect(ap(off)), ap(b), op))
+            issue("v", [a, b, off], [out], lambda: V.tensor_tensor(ap(out), ap(a).indirect(ap(off)), ap(b), op),
+                  time=0.05 + 0.0013 * width(out))
 
     def cp(out, in_):
         issue("v", [in_], [out], lambda: V.tensor_copy(ap(out), ap(in_)))
+
+    def turn(out, in_):
+        issue("v", [in_], [out], lambda: V.transpose(ap(out), ap(in_)))
 
     def ac(out, in_):
         issue("a", [in_], [out], lambda: A.activation(ap(out), ap(in_), F.Copy))
@@ -150,16 +235,19 @@ def rank_program(g, core, T, topo):
         issue("a", rs, [out], lambda: A.activation(ap(out), ap(in_), func, bias=num(bias), scale=scale))
 
     def gather(out, win, off):
-        issue("v", [win, off], [out], lambda: V.tensor_copy(ap(out), ap(win).indirect(ap(off))))
+        issue("v", [win, off], [out], lambda: V.tensor_copy(ap(out), ap(win).indirect(ap(off))),
+              time=0.05 + 0.0013 * width(out))
 
     def gather_a(out, win, off, scale=1.0):
-        issue("a", [win, off], [out], lambda: A.activation(ap(out), ap(win).indirect(ap(off)), F.Identity, scale=scale))
+        issue("a", [win, off], [out], lambda: A.activation(ap(out), ap(win).indirect(ap(off)), F.Identity, scale=scale),
+              time=0.065 + 0.0013 * width(out))
 
     def scatter(win, val, off):
-        issue("v", [val, off], [win], lambda: V.tensor_copy(ap(win).indirect(ap(off)), ap(val)))
+        issue("v", [val, off], [win], lambda: V.tensor_copy(ap(win).indirect(ap(off)), ap(val)), time=0.1)
 
     def scan(out, keep, add, op0=O.min, op1=O.add):
-        issue("v", [keep, add], [out], lambda: V.tensor_tensor_scan(ap(out), ap(keep), ap(add), 0.0, op0, op1))
+        issue("v", [keep, add], [out], lambda: V.tensor_tensor_scan(ap(out), ap(keep), ap(add), 0.0, op0, op1),
+              per=narrow(out, keep, add))
 
     corr = r("cn", 0, 1)
 
@@ -167,80 +255,87 @@ def rank_program(g, core, T, topo):
         scan(out, r("dq", a, b), val, O.add, O.max)
 
     def fill(x, c):
-        issue("v", [], [x], lambda: V.memset(ap(x), c))
-
-    def zero(x, src):
-        lin(x, src, 0.0, 0.0)
+        issue("v", [], [x], lambda: V.memset(ap(x), c), per=narrow(x))
 
     def both(name, a, b):
         return [r(name, a, b), r(name + "_s", a, b)]
 
     def qz(cod, o, n, tile):
         c, s = both(cod, o, o + n)
-        issue("v", [tile], [c, s], lambda: V.quantize_mx(mx(c), mx(s), ap(tile)))
+        issue("v", [tile], [c, s], lambda: V.quantize_mx(mx(c), mx(s), ap(tile)), time=0.012 + 0.00088 * n)
 
     def mm(k, lhs, lo, rhs, ro, n, start=True, stop=True):
         w, x, out = both(lhs, lo, lo + 128), both(rhs, ro, ro + n), r("ps%d" % k, 0, n)
         issue("t", w + x, [out], lambda: X.matmul_mx(ap(out), mx(w[0]), mx(w[1]), mx(x[0]), mx(x[1]), start, stop),
-              adds=not start)
+              adds=not start, time=0.00116 * (n + 16))
 
     def pick(dst, c, n, src, a, b, off, parts):
         do, so, wc, ws = r(dst, c, c + n), r(dst + "_s", c, c + n), r(src, a, b), r(src + "_s", a, b)
         issue("v", [r(src, x, y) for x, y in parts] + [off], [do], lambda: V.tensor_copy(
-            ap(do, dt.uint32), ap(wc, dt.uint32).indirect(ap(off))))
+            ap(do, dt.uint32), ap(wc, dt.uint32).indirect(ap(off))), time=0.05 + 0.0013 * n)
         issue("a", [r(src + "_s", x, y) for x, y in parts] + [off], [so], lambda: A.activation(
-            ap(so), ap(ws).indirect(ap(off)), F.Copy))
+            ap(so), ap(ws).indirect(ap(off)), F.Copy), time=0.065 + 0.0013 * n)
 
     def iota(x, pattern, base, cm):
         if SCRATCH[x[0]][2] == "int32":
-            issue("g", [], [x], lambda: g.iota(ap(x), pattern, base, cm))
+            issue("g", [], [x], lambda: g.iota(ap(x), pattern, base, cm), time=0.13 + 0.00166 * width(x))
         else:
-            issue("g", [], [x], lambda: g.iota(ap(x), pattern, base, cm, allow_small_or_imprecise_dtypes=True))
+            issue("g", [], [x], lambda: g.iota(ap(x), pattern, base, cm, allow_small_or_imprecise_dtypes=True),
+                  time=0.13 + 0.00166 * width(x))
 
-    def dma(q, out, in_, sem, total=16):
-        issue(q, [in_] if isinstance(in_, tuple) else [], [out] if isinstance(out, tuple) else [],
-              lambda: queue[q].dma_start(num(out), num(in_)), sem, total)
+    def choose(out, in_, pattern, op, other, base, cm):
+        issue("g", [in_], [out], lambda: g.affine_select(ap(out), ap(in_), pattern, op, other, base, cm),
+              time=0.17 + 0.00166 * width(out))
 
-    def move(dst, a, src, b, n, sem, total=32):
+    def dma(q, out, in_, sem, total=16, behind=(), time=0.8):
+        issue(q, ([in_] if isinstance(in_, tuple) else []) + list(behind), [out] if isinstance(out, tuple) else [],
+              lambda: queue[q].dma_start(num(out), num(in_)), sem, total, time=time)
+
+    def move(dst, a, src, b, n, sem, total=32, behind=()):
         for x, y in zip(both(dst, a, a + n), both(src, b, b + n)):
-            dma("s", x, y, sem, total)
-
-    def idle():
-        pass
+            dma("s", x, y, sem, total, behind)
 
     sh = me % 2
     e6, em = (sh, sh + 6), me + sh
-
     others = [x for x in range(N) if x != me]
 
-    def far_of(x):
-        return [y for y in range(N) if topo.chip(T.cores[y]) != topo.chip(T.cores[x])]
-    far = far_of(me)
-    near = [x for x in others if x not in far]
+    def slot(x, y):
+        return HX + TH * (2 + near_of(x).index(y))
+    far, near, mate = far_of(me), near_of(me), mate_of(me)
     all_eng = topo.engines(core, T.cores[near[0]])
     out_eng = topo.engines(core, T.cores[far[0]])
     in_eng = [e for e in all_eng if e not in out_eng]
 
-    def third(x):
-        return [y for y in range(N) if y not in far_of(x)].index(x)
-    mate = [x for x in far if third(x) == third(me)][0]
-
     def mask(es):
         return sum(1 << e for e in es)
 
-    def dst(x):
-        a = topo.addr(T.cores[x])
-        return DstId(rid=a[0], pnc=a[1])
+    lands, sent = {}, []
 
-    def send(transfers, src):
-        before("g", [src], [])
+    def send(transfers, src, behind=()):
+        ops.append(("g", [src] + list(behind), [], 0.25, 0.25, sent[-1:]))
+        calls.append(lambda: remote(transfers, [src] + list(behind)))
+        sent.append(len(ops) - 1)
+        for sem in sorted(set(e[4] for e in transfers), key=lambda s: s == "an"):
+            ops.append(("x", [], lands[sem], 0.0, 1.3 if len(sent) > 1 else 2.4, sent[-1:]))
+            calls.append(lambda: None)
+
+    def remote(transfers, reads):
+        before("g", reads, [])
         due["left"] = due.get("left", 0) + sum(len(e[1]) for e in transfers)
-        g.remote_dma_fused([RemoteDMATransfer(dst_ids=[dst(y) for y in x], dma_engine_mask=mask(es), remote_sem=T.sem[sem],
+        g.remote_dma_fused([RemoteDMATransfer(dst_ids=[address(y) for y in x], dma_engine_mask=mask(es), remote_sem=T.sem[sem],
                                               srcs=[ap(s)], dsts=[ap(to)] * len(x)) for x, es, s, to, sem in transfers],
                            local_sem=T.sem["left"])
 
-    def spread(src, to, sem, sem2=None):
-        send([(far, out_eng, src, to, sem), (near, in_eng, src, to, sem2 or sem)], src)
+    def spread(src, sem, sem2=None):
+        send([([T.cores[x] for x in far], out_eng, src, src, sem), ([T.cores[x] for x in near], in_eng, src, src, sem2 or sem)],
+             src)
+
+    def to_mate(k):
+        src = both("hp", 0, TH)[k]
+        if helper(me) is None:
+            send([([T.cores[mate]], out_eng, src, both("hp", TH, 2 * TH)[k], "ah")], src)
+        else:
+            send([([helper(me)], in_eng, src, both("hr", 0, TH)[k], "r%d" % k)], src)
 
     h_all = len(all_eng) // 2
     n_all = sum(len(out_eng) if x in far else len(in_eng) for x in others)
@@ -248,297 +343,251 @@ def rank_program(g, core, T, topo):
                                          ("ax", 2 * len(out_eng) * len(far), far, "w0", lambda x: LX + K * x, K),
                                          ("an", 2 * len(in_eng) * len(near), near, "w0", lambda x: LX + K * x, K),
                                          ("ah", 2 * len(out_eng), [mate], "hp", lambda x: TH, TH),
-                                         ("a3", 2 * h_all * len(near), near, "w0", lambda x: HX + TH * third(x), TH)):
+                                         ("a3", 2 * h_all * len(near), near, "w0", lambda x: slot(me, x), TH)):
         due[sem] = tot
         for x in whom:
             for e in both(buf, base(x), base(x) + w):
                 wrote(e, (sem, tot))
+                lands.setdefault(sem, []).append(e)
     due["am"] = n_all
+    lands["r0"] = lands["r1"] = lands["ah"]
     for x in others:
         wrote(r("land", 8 * x, 8 * x + 1), ("am", n_all))
+        lands.setdefault("am", []).append(r("land", 8 * x, 8 * x + 1))
 
-    dma("a", r("ut"), T.u[:, 0:4], "du")
+    dma("a", r("ut"), T.u[:, 0:4], "du", time=0.6)
     dma("s", r("tbt"), T.tb[:, :], "dtb")
-    dma("s", r("nzt", 0, 384), T.nz[:, :], "dnz", 32)
-    dma("s", r("nzt", 384, 704), T.nz[:, 0:320], "dnz", 32)
-    dma("s", r("vt", 192, 512), T.tb[:, 0:320], "dpv")
-    dma("s", r("wt"), T.w[:, :], "dw")
+    for buf in ("ct", "vn"):
+        dma("s", r(buf, 0, 384), T.u[:, 128:512], "d" + buf, 32, [r("tbt")] if buf == "vn" else [], time=1.3)
+        dma("s", r(buf, 384, 768), T.u[:, 128:512], "d" + buf, 32, time=1.3)
+    dma("s", r("nzt", 0, 384), T.nz[:, :], "dnz", 32, time=2.0)
+    dma("s", r("nzt", 384, 704), T.nz[:, 0:320], "dnz", 32, time=2.0)
+    dma("s", r("vt", 192, 512), T.tb[:, 0:320], "dpv", time=2.0)
+    dma("s", r("wt"), T.w[:, :], "dw", time=2.6)
 
     six = (0, 6)
-    iota(r("pi"), [[0, 2]], 0, 1)
+    iota(r("pi"), [[16 - sh, 2], [0, 2]], 0, 1)
+    iota(r("pf"), [[64, 2]], 0, 1)
     iota(r("ipd"), [[1, 128]], 0, -1)
     iota(r("t16"), [[0, 12], [1, 16]], 0, 0)
-    iota(r("irb"), [[1, 192]], 0, 0)
+    iota(r("t16", 0, 192, 16), [[0, 12]], -1000, 0)
+    iota(r("irb"), [[1, 192], [0, 2]], 0, 0)
     iota(r("ir"), [[1, 8]], 0, 0)
-    iota(r("hq"), [[0, 16]], 0, 0)
     iota(r("m16"), [[16, 4]], 0, 0)
-    iota(r("n6"), [[16, 6]], 0, 0)
-    iota(r("c48"), [[48, 8]], 0, 0)
+    iota(r("dl"), [[16, 2], [32, 2], [0, 2]], 0, 0)
     iota(r("rke"), [[1, 16]], -sh, 0)
+    iota(r("n16"), [[0, 6], [16, 16]], 0, 0)
+    iota(r("c48"), [[48, 8]], 0, 0)
     iota(r("cnx"), [[16, 12]], NX, 0)
-    iota(r("hq", *e6), [[0, N // len(far)], [TH, len(far)]], HX - 2 * K, 0)
+    iota(r("hq"), [[0, 16]], 0, 0)
+    iota(r("fb"), [[0, 16]], 0, 0)
+    iota(r("key"), [[0, 16]], -100, 0)
+    iota(r("tm"), [[0, 64]], 0, 0)
+    iota(r("ones"), [[0, 32]], 1, 0)
+    iota(r("i16"), [[0, 2], [1, 16]], 0, 0)
     iota(r("x48"), [[0, 6], [1000, 48]], 0, 0)
+    for x in [me] + near:
+        a, b = (HX, HX + TH) if x == me else (slot(me, x),) * 2
+        if mate_of(x) < x:
+            a, b = b, a
+        lo, step = min(x, mate_of(x)) + sh, abs(x - mate_of(x))
+        iota(r("hq", lo, lo + step + 1, step), [[b - a, 2]], a - 2 * K, 0)
 
-    fill(r("ones"), 1.0)
-    fill(r("onet"), 1.0)
-    zero(r("ct", 0, 512), r("onet", 0, 512))
-    ts(r("pa", 0, 2), r("pi"), 64, O.bitwise_and)
-    ts(r("pa", 2, 4), r("pi"), 4, O.arith_shift_right)
-    ts(r("pa", 4, 6), r("pi"), 15, O.bitwise_and)
-    qz("oneq", 0, 128, r("onet", 0, 512))
+    fill(r("half"), 0.5)
+    choose(r("eht"), r("half"), [[1, 516]], O.is_equal, 0.0, -3, -4)
+    choose(r("rsq"), r("ones"), [[0, 2], [1, 16]], O.not_equal, 0.0, 0, 0)
+    ts(r("pa", 0, 4), r("pi"), 15, O.bitwise_and)
+    ts(r("pa", 4, 6), r("pi", 0, 2), 1, O.bitwise_and)
+    qz("oneq", 0, 128, r("half", 0, 512))
     cp(r("paf"), r("pa"))
-    own = r("paf", 4, 5)
-    ts(r("bm"), r("ipd"), 0.0, O.is_le, 3e29, O.mult)
-    for k, (a, b) in enumerate(((7.5, 1.0), (11.5, -5.0), (12.5, 4.0))):
-        ts(r("pio", k, k + 1), own, a, O.is_gt, b, O.mult)
-    zero(r("ct", 512, 768), r("onet", 0, 256))
+    own = r("paf", 0, 1)
+    lin(r("bm"), r("ipd"), -3e29, 1.5e29, F.Relu)
+    ts(r("dm"), r("i16"), own, O.is_equal)
+    ts(r("cn", 2, 3), r("paf", 2, 3), -3.0, O.add, 2.5, O.max)
+    for k in range(2):
+        lin(r("cn", 16 + k, 17 + k), own, -1.0, r("pf", k, k + 1))
+        lin(r("wct", k, 512, 4), r("half", 0, 128), 0.0, own)
+        lin(r("wct", 2 + k, 512, 4), r("half", 0, 128), 0.0, r("cn", 16 + k, 17 + k))
     for k in range(4):
         if k % 2:
-            lin(r("ubt", k, 512, 4), r("ones"), 0.0, r("ut", k, k + 1))
+            lin(r("ubt", k, 512, 4), r("half", 0, 128), 0.0, r("ut", k, k + 1))
         else:
-            ts(r("ubt", k, 512, 4), r("onet", 0, 128), r("ut", k, k + 1), O.mult)
-    lin(r("cn", 16, 17), r("paf", 2, 3), 16.0, 0.0)
-    lin(r("cn", 17, 18), r("paf", 2, 3), 16.0, 64.0)
-    lin(r("t16", 0, 192, 16), r("ones", 0, 12), 0.0, -1000.0)
-    lin(r("cn", 1, 2), own, 1.0, 0.5)
-    lin(r("cn", 10, 11), r("paf", 0, 1), -4.0, 256.0)
-    lin(r("cn", 11, 12), r("paf", 0, 1), 4.0, 0.0)
-    for k in range(2):
-        lin(r("wct", 512 + k, 1024, 2), r("onet", 0, 256), 0.0, r("cn", 16 + k, 17 + k))
+            ts(r("ubt", k, 512, 4), r("half", 0, 128), r("ut", k, k + 1), O.mult, 2.0, O.mult)
+    lin(r("cn", 1, 2), own, -STEP, -STEP / 2)
     qz("uq", 0, 128, r("ubt"))
+    lin(corr, own, 32.0, -480.0, F.Square)
+    lin(r("nr8", *six), r("ir", *six), -0.125, 0.0)
+    lin(r("nc8", *six), r("ir", *six), -0.125, corr)
+    lin(r("cn", 5, 6), own, 32.0, -32.0 * (sh + 5), F.Square)
+    lin(r("nw", 0, 3), r("m16", 0, 3), 1.0, own)
+    lin(r("cn", 3, 4), r("cn", 5, 6), 1.0, corr)
+    lin(r("nws", 0, 3), r("nw", 0, 3), 1.0 / K, 0.0)
+    lin(r("cn", 9, 10), r("paf", 4, 5), 61.0, 2.0)
+    lin(r("cn", 6, 7), corr, 1.0, float(K))
+    lin(r("v1r"), r("rke"), 16.0, own)
+    lin(r("n16"), r("n16"), 1.0, own)
+    lin(r("cnx"), r("cnx"), 1.0, own)
+    lin(r("cn", 4, 5), own, 3.0, r("cn", 9, 10))
+    lin(r("dq"), r("t16"), STEP, r("cn", 1, 2))
+    cp(r("l6"), r("ir", *six))
+    ts(r("odl"), r("dl"), own, O.add)
+    qz("oneq", 128, 128, r("wct"))
+    for k in range(4):
+        qz("eq", 128 * k, 128, r("eht", 3 - k, 515 - k))
+    qz("nq", 0, 176, r("nzt"))
+    qz("wq", 0, 256, r("wt"))
 
     qz("tq", 0, 192, r("tbt"))
     mm(0, "uq", 0, "tq", 0, 192)
     mm(1, "tq", 0, "uq", 0, 128)
     mm(2, "tq", 64, "uq", 0, 128)
     mm(6, "uq", 0, "tq", 0, 192)
-    ts(r("wct", 0, 512), r("onet", 0, 512), own, O.mult)
     move("lb", K, "tq", K, 80, "dpad", 32)
 
     lin(r("sg"), r("ps6", 0, 192), 1.0, 0.0, F.Sign)
-    zero(r("vn", 0, 512), r("onet", 0, 512))
     issue("a", [r("sg")], [r("sg1"), r("msgf", 0, 1)], lambda: A.activation(
         ap(r("sg1")), ap(r("sg")), F.Relu, accum_out=ap(r("msgf", 0, 1))))
-    lin(corr, own, 32.0, -480.0, F.Square)
-    zero(r("vn", 512, 768), r("onet", 0, 256))
-    zero(r("eht"), r("onet"))
-    lin(r("nr8", *six), r("ir", *six), -0.125, 0.0)
-    lin(r("key"), r("ones", 0, 16), 0.0, -100.0)
-    lin(r("nc8", *six), r("ir", *six), -0.125, corr)
-    lin(r("cn", 14, 15), own, 1.0, -6.0, F.Relu)
-    lin(r("cn", 5, 6), own, 32.0, -32.0 * (sh + 5), F.Square)
-    lin(r("nw", 0, 3), r("m16", 0, 3), 1.0, own)
 
     def lower(src, a=0, b=192):
         return r(src, a, b, 1, 64, 128)
 
-    def gt_ops(src, sp0, sp1):
-        return [lambda: ts(r("ct", 0, 512, 4), r(src, 0, 128), sp0, O.is_gt),
-                lambda: ts(r("ct", 512, 768, 4), r(src, 128, 192), sp0, O.is_ge),
-                lambda: ts(r("ct", 1, 768, 4, 64), lower(src), sp1, O.is_gt)]
-
-    def tie0(sp0):
-        ts(r("ct", 2, 512, 4), r("sm"), sp0, O.is_equal)
-
-    def low1(src):
+    def compare(src, sp0, sp1, all_):
         tt(r("sm1", 0, 64, 1, 64), lower(src, 128), r("bm", 64, 128, 1, 64), O.add)
+        ts(r("ct", 0, 512, 4), r(src, 0, 128), sp0, O.is_gt, 2.0, O.mult)
+        ts(r("ct", 512, 768, 4), r(src, 128, 192), sp0, O.is_ge, 2.0, O.mult)
+        if all_:
+            ts(r("ct", 1, 768, 4, 64), lower(src), sp1, O.is_gt, 2.0, O.mult)
+        ts(r("ct", 2, 512, 4), r("sm"), sp0, O.is_equal, 2.0, O.mult)
+        ts(r("ct", 515, 768, 4, 64), r("sm1", 0, 64, 1, 64), sp1, O.is_equal, 2.0, O.mult)
+        qz("cq", 0, 192, r("ct"))
 
-    def tie1(sp1):
-        ts(r("ct", 515, 768, 4, 64), r("sm1", 0, 64, 1, 64), sp1, O.is_equal)
+    def listed(out, a, b, src):
+        select(r("sc2", a, b), src, a, b)
+        ts(out, r("sc2", a + 15, b, 16), corr, O.subtract)
 
-    def order_ops(out, a, b, src):
-        return [lambda: select(r("sc2", a, b), src, a, b),
-                lambda: ts(out, r("sc2", a + 15, b, 16), corr, O.subtract)]
-
-    s0, s1 = r("ps1", 0, 1), r("ps2", 0, 1, 1, 64)
-    gts = gt_ops("ps0", s0, s1)
     tt(r("sm"), r("ps0", 0, 128), r("bm"), O.add)
-    low1("ps0")
-    gts[0]()
-    gts[1]()
-    tie0(s0)
-    gts[2]()
-    tie1(s1)
-    qz("cq", 0, 192, r("ct"))
+    compare("ps0", r("ps1", 0, 1), r("ps2", 0, 1, 1, 64), True)
     mm(4, "cq", 0, "oneq", 0, 128)
     mm(5, "cq", 64, "oneq", 0, 128)
-    qz("oneq", 128, 256, r("wct"))
 
-    def hot(a, b):
-        ts(r("vn", 4 * a, 4 * b, 4), r("irb", a, b), r("ps4", 0, 1), O.is_equal)
-        ts(r("vn", 4 * a + 1, 4 * b, 4, 64), r("irb", a, b, 1, 64), r("ps5", 0, 1, 1, 64), O.is_equal)
-
-    def order(k, a):
-        qz("cq", a, 128, r("vn", 4 * a, 4 * a + 512))
-        mm(k, "oneq", 128, "cq", a, 128, True, False)
-        mm(k, "oneq", 256, "cq", a, 128, False, True)
+    def order(k, a, b, n):
+        ts(r("vn", 4 * a, 4 * b, 2), r("irb", 2 * a, 2 * b), r("ps4", 0, 1), O.is_equal)
+        ts(r("vn", 4 * a + 1, 4 * b, 2, 64), r("irb", 2 * a, 2 * b, 1, 64), r("ps5", 0, 1, 1, 64), O.is_equal)
+        qz("cq", a, n, r("vn", 4 * a, 4 * a + 4 * n))
+        mm(k, "oneq", 128, "cq", a, n)
 
     my_land = r("land", 8 * me, 8 * me + 1)
-    ts(r("msgf", 1, 2), r("msgf", 0, 1), r("cn", 10, 11), O.mult, r("ps4", 0, 1), O.add)
-    hot(0, 128)
-    ts(my_land, r("ps5", 0, 1), r("cn", 11, 12), O.mult, r("msgf", 1, 2), O.add)
-    spread(my_land, my_land, "am")
-    order(3, 0)
-    ts(r("dq"), r("t16"), r("cn", 1, 2), O.subtract, STEP, O.mult)
-    hot(128, 192)
-    low = order_ops(r("ol", 0, 3), 0, 48, r("ps3", 0, 48))
-    low[0]()
-    ts(r("idt"), r("ipd"), 0.0, O.is_equal, 0.5, O.mult)
-    low[1]()
-    ts(r("cn", 12, 13), own, sh + 5.5, O.is_gt, 0.5, O.mult)
-    ts(r("cn", 13, 14), own, sh - 0.5, O.is_lt, 0.5, O.mult)
-    pick("ls", 0, 48, "tq", 0, 192, r("ol", 0, 3), [(0, 192)])
-    for x, y in zip(both("ls", 0, K), both("w0", K * me, K * me + K)):
-        spread(x, y, "al")
-    move("w0", K * me, "ls", 0, K, "dls")
-
-    order(2, 64)
-    ac(r("eht", 3, 515, 4), r("idt"))
-    lin(r("cn", 15, 16), r("cn", 12, 13), 1.0, r("cn", 13, 14))
-    lin(r("cn", 14, 15), r("cn", 14, 15), 1.0, 2.5)
-    lin(r("cn", 3, 4), r("cn", 5, 6), 1.0, corr)
-    lin(r("nws", 0, 3), r("nw", 0, 3), 1.0 / K, 0.0)
-    lin(r("cn", 2, 3), r("cn", 14, 15), 1.0, r("cn", 15, 16))
-    lin(r("cn", 4, 5), own, 6.0, 0.0)
-    lin(r("cn", 6, 7), corr, 1.0, float(K))
-    lin(r("cn", 7, 8), r("ones", 0, 1), 0.0, 0.5 - K)
-    lin(r("cn", 8, 9), r("ones", 0, 1), 0.0, 0.5 - 2 * K)
-    weave([lambda: fill(r("fb"), 0)], order_ops(r("om", 0, 3), 48, 96, r("ps3", 48, 96)),
-          [lambda k=k: tt(r("pio", 3, 4), r("pio", k, k + 1), r("pio", 3, 4) if k else own, O.add) for k in range(3)],
-          [lambda: qz("nq", 0, 176, r("nzt"))], order_ops(r("ol", 6, 12), 96, 192, r("ps2", 32, 128)))
-    pick("nb", 0, 48, "tq", 0, 192, r("om", 0, 3), [(0, 192)])
+    ts(r("land", 8 * me, 8 * me + 1, 1, 0, 64), r("msgf", 0, 1, 1, 0, 64), 256.0, O.mult, r("ps4", 0, 1, 1, 0, 64), O.add)
+    ts(r("land", 8 * me, 8 * me + 1, 1, 64), r("ps5", 0, 1, 1, 64), 256.0, O.mult, r("ps4", 0, 1, 1, 64), O.add)
+    spread(my_land, "am")
+    order(3, 0, K, 128)
+    listed(r("ol", 0, 3), 0, 48, r("ps3", 0, 48))
+    pick("w0", K * me, K, "tq", 0, 192, r("ol", 0, 3), [(0, 192)])
+    for x in both("w0", K * me, K * me + K):
+        spread(x, "al")
+    order(2, K, P, P - K)
+    listed(r("om", 0, 3), 48, 96, r("ps2", 0, 48))
+    listed(r("ol", 6, 12), 96, 192, r("ps2", 48, 144))
+    pick("w0", PAD, HX - PAD, "tq", 0, 192, r("ol", 0, 1), [(0, 192)])
     pick("hp", 0, TH, "tq", 0, 192, r("ol", 6, 12), [(0, 192)])
-    lin(r("hq", mate + sh, mate + sh + 1), r("ones", 0, 1), 0.0, float(HX + TH * 3 - 2 * K))
-    lin(r("v1r"), r("rke"), 16.0, r("pio", 3, 4))
-    lin(r("cn", 9, 10), r("pio", 3, 4), 1.0, 16.0 * me)
-    lin(r("rsq"), r("x48", 0, 32), 0.0, 1.0)
-    lin(r("cnx"), r("cnx"), 1.0, own)
-    lin(r("rho", 84, 96), r("ones", 0, 12), 0.0, 0.0)
-    lin(r("rsq", 0, 32, 16), r("ones", 0, 2), 0.0, 0.0)
-
-    def unit(k):
-        qz("eq", 128 * k, 128, r("eht", 3 - k, 515 - k))
+    to_mate(0)
+    to_mate(1)
+    pick("nb", 0, 48, "tq", 0, 192, r("om", 0, 3), [(0, 192)])
 
     def noise(t, stop):
         for k in range(4):
             mm(4 + k, "eq", 128 * k, "nq", K * t, 128, True, stop)
+    noise(0, False)
 
     def places(k, ref, val, zr):
         pu, tpu = r("pt", 4 * k, 4 * k + 1), r("pt", 4 * k + 2, 4 * k + 3)
         pl, t5 = r("pl", k, k + 1), r("t5", k, k + 1)
         issue("a", [r("k2", *six), ref], [r("gt", *six), pl], lambda: A.activation(
-            ap(r("gt", *six)), ap(r("k2", *six)), F.Sign, bias=ap(ref), scale=-1.0, accum_out=ap(pl)))
+            ap(r("gt", *six)), ap(r("k2", *six)), F.Sign, bias=ap(ref), scale=-1.0, accum_out=ap(pl)), time=0.155)
         ts(pu, pl, -0.5, O.mult, r("cn", 2, 3), O.add)
         ts(t5, pl, -1.0, O.mult, pl, O.max)
         scatter(r("wr%d" % k), val, pu)
         ts(tpu, t5, -0.5, O.mult, 2.5, O.add)
-        if k:
-            scatter(r("wb"), r("b32"), pu)
         gather(zr, r("wr%d" % k), tpu)
+        lin(r("odt", 6 * k, 6 * k + 6), r("wr%d" % k, *six), 1.0 / 16 if k else 1.0, 0.0)
         return pu, tpu
 
-    def note(k, scale):
-        lin(r("odt", 6 * k, 6 * k + 6), r("wr%d" % k, *six), scale, 0.0)
-
-    def anew(buf, off, parts, end):
-        pick(buf, 0, 48, "w0", 0, end, off, parts)
-        for k in range(4):
-            mm(4 + k, "eq", 128 * k, buf, 0, 128, False, True)
-
-    def pack_ops(out, o):
-        return [lambda k=k: (cp if k % 2 else ac)(r("vt", k, 192, 4), r("ps%d" % (4 + k), 0, 48)) for k in range(4)] + [
-            lambda: qz(out, o, 128, r("vt"))]
-
-    unit(0)
-    unit(1)
-    unit(2)
-    cp(r("l6"), r("ir", *six))
-    ts(r("ia"), r("ipd", 0, 32), 15, O.bitwise_and)
-    ts(r("hi", *six), r("land", 0, 48, 8), 1.0 / 256, O.mult, -127.5 / 256, O.add)
-    issue("g", [r("hi", *six)], [r("fb", *e6)], lambda: g.partition_broadcast(
-        ap(r("fb", *e6)), ap(r("hi", 0, 6, 1, 0, 1)), 128))
-    cp(r("v6", *six), r("land", 0, 48, 8))
-    unit(3)
-    noise(0, False)
-    ts(r("dm"), r("ia"), 0.0, O.is_equal)
+    for k in (0, 64):
+        ts(r("fb", sh, sh + 6, 1, k, k + 64), r("land", 0, 48, 8, 0, 64), 1.0 / 256, O.mult, -127.5 / 256, O.add)
     tt(r("key", *e6), r("fb", *e6), r("nr8", *six), O.add)
     tt(r("k2", *six), r("fb", *e6), r("nc8", *six), O.add)
     select(r("ks"), r("key"), 0, 16)
-    qz("wq", 0, 256, r("wt"))
     pu, tpu = places(0, r("ks", 15, 16), r("rke"), r("zr0"))
-    scatter(r("wf"), r("fb"), pu)
     ts(r("oll", 0, 3), r("nws", 0, 3), r("zr0", em, em + 1), O.add, float(K), O.mult)
-    cp(r("rw", 48, 54), r("v6", *six))
 
-    for k in range(8):
-        dma("s", ("mdr", 0, 16, 6 * k, 6 * k + 6, 1), r("v6", 0, 6, 1, 16 * k, 16 * k + 16), "dmd", 128)
-    for k in range(8):
-        dma("s", r("rw", 0, 48, 1, 16 * k, 16 * k + 16), ("mdr", 0, 16, 0, 48, 1), "drw", 128)
+    ts(r("hi", *six), r("land", 0, 48, 8), 1.0 / 256, O.mult, -127.5 / 256, O.add)
+    cp(r("vf", *six), r("land", 0, 48, 8))
+    cp(r("hf", *six), r("hi", *six))
+    ts(r("h2", *six), r("hf", *six), -256.0, O.mult)
+    tt(r("rho", 2, 8), r("h2", *six), r("vf", *six), O.add)
+    for k in range(6):
+        src = r("rho", 2, 8, 1, 32 * k, 32 * k + 32) if k < 4 else r("hf", 0, 6, 1, 32 * k - 64, 32 * k - 32)
+        ac(r("tm", 6 * k, 6 * k + 6, 1, 0, 32), src)
+    for k in (32, 64):
+        cp(r("tm", 0, 36, 1, k, 2 * k), r("tm", 0, 36, 1, 0, k))
+    turn(r("t1"), r("tm"))
+    gather(r("t2"), r("t1"), r("odl"))
+    turn(r("rho", 8, 136), r("t2"))
+    ac(r("rho", 66, 72), r("hf", *six))
 
+    pick("lb", 0, 48, "w0", 0, 288, r("oll", 0, 3), [(0, 288)])
+    for k in range(4):
+        mm(4 + k, "eq", 128 * k, "lb", 0, 128, False, True)
     ts(r("tk", 0, 1), r("zr0", em, em + 1), float(me), O.not_equal, 64.0, O.mult)
-    anew("lb", r("oll", 0, 3), [(0, 288)], 288)
-    note(0, 1.0)
     ts(r("ox", 0, 3), r("nw", 0, 3), r("tk", 0, 1), O.add)
-    gather(r("fa"), r("wf"), tpu)
-    scatter(r("wc"), r("hq"), pu)
-    tt(r("t0", *six), r("zr0", *e6), r("ir", *six), O.not_equal)
-    ts(r("ob"), r("zr0", *e6), r("cn", 4, 5), O.add)
-    gather(r("cz"), r("wc"), tpu)
-    weave(pack_ops("nb", 64))
-    pick("xs", 0, 48, "nb", 0, 192, r("ox", 0, 3), [(0, 48), (64, 192)])
-    for x, y in zip(both("xs", 0, K), both("w0", LX + K * me, LX + K * me + K)):
-        spread(x, y, "ax", "an")
-    move("w0", LX + K * me, "xs", 0, K, "dxs")
+    for k in range(4):
+        (cp if k else ac)(r("vt", k, 192, 4), r("ps%d" % (4 + k), 0, 48))
+    qz("nb", 64, 128, r("vt"))
+    pick("w0", LX + K * me, K, "nb", 0, 192, r("ox", 0, 3), [(0, 48), (64, 192)])
+    for x in both("w0", LX + K * me, LX + K * me + K)[::-1]:
+        spread(x, "ax", "an")
     noise(1, True)
     mm(1, "uq", 0, "w0", 0, 288)
 
-    fit = [
-        lambda: lin(r("r96", *six), r("fa", *e6), 1.0, float(K - P + K), F.Relu),
-        lambda: lin(r("r144", *six), r("fa", *e6), 1.0, float(K - P), F.Relu),
-        lambda: tt(r("fan", *six), r("fa", *e6), r("nr8", *six), O.add),
-        lambda: tt(r("u1", *six), r("r96", *six), r("r144", *six), O.subtract),
-        lambda: tt(r("v1", *six), r("u1", *six), r("r144", *six), O.subtract),
-        lambda: tt(r("fan", *six), r("fan", *six), r("u1", *six), O.subtract),
-        lambda: tt(r("v1", *six), r("v1", *six), r("t0", *six), O.mult),
-        lambda: tt(r("key", *e6), r("fan", *six), r("v1", *six), O.add),
-        lambda: select(r("ks"), r("key"), 0, 16),
-        lambda: ts(r("ap3", *six), r("key", *e6), r("ks", 15, 16), O.subtract, r("cn", 3, 4), O.add)]
-    bases = [
-        lambda: lin(r("c1", *six), r("t0", *six), float(LX), 0.0),
-        lambda: lin(r("bz", *six), r("zr0", *e6), float(K), float(LX - K)),
-        lambda: tt(r("c1", *six), r("c1", *six), r("c48", *six), O.add),
-        lambda: tt(r("hc2", *six), r("cz", *e6), r("bz", *six), O.subtract),
-        lambda: tt(r("hb2", *six), r("bz", *six), r("c1", *six), O.subtract),
-        lambda: tt(r("cb", *six), r("cz", *e6), r("c1", *six), O.add),
-        lambda: gather_a(r("hc"), r("hc2"), r("l6"), 0.5),
-        lambda: gather_a(r("hb"), r("hb2"), r("l6"), 0.5),
-        lambda: gather_a(r("ca"), r("cb"), r("l6"), 0.5),
-        lambda: ts(r("bzf"), r("zr0"), *((min(far) - 0.5, O.is_gt) if me < min(far) else (max(far) + 0.5, O.is_lt)), TH, O.mult)]
-    where = [
-        lambda: ts(r("hw"), r("rw"), 1.0 / 256, O.mult, -127.5 / 256, O.add),
-        lambda: cp(r("vf"), r("rw")),
-        lambda: ts(r("h2"), r("hw"), -256.0, O.mult),
-        lambda: cp(r("rho", 54, 84), r("hw", 24, 54)),
-        lambda: tt(r("rho", 0, 54), r("h2"), r("vf"), O.add),
-        lambda: gather_a(r("rg"), r("rho"), r("ob")),
-        lambda: tt(r("yt"), r("rho"), r("ca"), O.add, r("ob")),
-        lambda: lin(r("sb"), r("rg"), 1.0, r("cn", 7, 8), F.Sign),
-        lambda: lin(r("sd"), r("rg"), 1.0, r("cn", 8, 9), F.Sign),
-        lambda: lin(r("b32"), r("bzf"), 1.0, own),
-        lambda: ac(r("sw", 0, 288), r("ps1", 0, 288)),
-        lambda: tt(r("sb"), r("sb"), r("hb"), O.mult),
-        lambda: tt(r("sd"), r("sd"), r("hc"), O.mult),
-        lambda: tt(r("yt"), r("yt"), r("sb"), O.add),
-        lambda: tt(r("y0g"), r("yt"), r("sd"), O.add)]
-    weave(bases, fit, [idle] * 5 + where[:5])
-    for q in ("g", "s"):
-        before(q, [r("hc2", *six)], [])
-    for x, y in zip(both("hp", 0, TH), both("hp", TH, 2 * TH)):
-        send([([mate], out_eng, x, y, "ah")], x)
-    move("w0", HX + TH * third(me), "hp", 0, TH, "dhb", 64)
-    move("w0", HX + TH * 3, "hp", TH, TH, "dhb", 64)
-    weave(where[5:])
-    lin(r("sw", HX, NX + 8), r("onet", 0, 392), 0.0, BIG)
+    scatter(r("wf"), r("fb"), pu)
+    gather(r("fa"), r("wf"), tpu)
+    scatter(r("wc"), r("hq"), pu)
+    gather(r("cz"), r("wc"), tpu)
+    tt(r("t0", *six), r("zr0", *e6), r("ir", *six), O.not_equal)
+    ts(r("ob"), r("zr0", *e6), r("cn", 4, 5), O.add)
+    lin(r("r96", *six), r("fa", *e6), 1.0, float(K - P + K), F.Relu)
+    lin(r("r144", *six), r("fa", *e6), 1.0, float(K - P), F.Relu)
+    tt(r("fan", *six), r("fa", *e6), r("nr8", *six), O.add)
+    tt(r("u1", *six), r("r96", *six), r("r144", *six), O.subtract)
+    tt(r("v1", *six), r("u1", *six), r("r144", *six), O.subtract)
+    tt(r("fan", *six), r("fan", *six), r("u1", *six), O.subtract)
+    tt(r("v1", *six), r("v1", *six), r("t0", *six), O.mult)
+    tt(r("key", *e6), r("fan", *six), r("v1", *six), O.add)
+    select(r("ks"), r("key"), 0, 16)
+    ts(r("ap3", *six), r("key", *e6), r("ks", 15, 16), O.subtract, r("cn", 3, 4), O.add)
+    lin(r("c1", *six), r("t0", *six), float(LX), 0.0)
+    lin(r("bz", *six), r("zr0", *e6), float(K), float(LX - K))
+    tt(r("c1", *six), r("c1", *six), r("c48", *six), O.add)
+    tt(r("hc2", *six), r("cz", *e6), r("bz", *six), O.subtract)
+    tt(r("hb2", *six), r("bz", *six), r("c1", *six), O.subtract)
+    tt(r("cb", *six), r("cz", *e6), r("c1", *six), O.add)
+    gather_a(r("hc"), r("hc2"), r("l6"), 0.5)
+    gather_a(r("hb"), r("hb2"), r("l6"), 0.5)
+    gather_a(r("ca"), r("cb"), r("l6"), 0.5)
+    ts(r("bzf", *six), r("zr0", *e6), *((min(far) - 0.5, O.is_gt) if me < min(far) else (max(far) + 0.5, O.is_lt)), TH, O.mult)
+    tt(r("y1g"), r("bzf"), r("n16"), O.add, r("l6"))
+    gather_a(r("rg"), r("rho"), r("ob"))
+    tt(r("yt"), r("rho"), r("ca"), O.add, r("ob"))
+    lin(r("sb"), r("rg"), 1.0, 0.5 - K, F.Sign)
+    lin(r("sd"), r("rg"), 1.0, 0.5 - 2 * K, F.Sign)
+    ac(r("sw", 0, 288), r("ps1", 0, 288))
+    tt(r("sb"), r("sb"), r("hb"), O.mult)
+    tt(r("sd"), r("sd"), r("hc"), O.mult)
+    tt(r("yt"), r("yt"), r("sb"), O.add)
+    tt(r("y0g"), r("yt"), r("sd"), O.add)
+    ts(r("yc"), r("y0g"), float(PAD), O.min)
+    move("w0", HX, "hp", 0, 2 * TH, "dhb", 32, both("w0", LX + K * min(far), LX + K * max(far) + K))
+    lin(r("sw", PAD, HX), r("ones", 0, 16), 0.0, BIG)
     for k in range(4):
         ac(r("dn", K * k, K * k + K), r("ps%d" % (4 + k), 0, K))
 
@@ -551,84 +600,68 @@ def rank_program(g, core, T, topo):
     scan(r("ks", *six), r("dq", *e6), r("psc", 47, 288, 48), O.add, O.max)
     tt(r("k2", *six), r("psc", 47, 288, 48), r("ap3", *six), O.add)
     pu, tpu = places(1, r("ks", 5, 6), r("v1r"), r("zg"))
-    og, ofs = r("zg", em, em + 1), r("osl", 0, 12)
-    gather(r("bzf"), r("wb"), tpu)
-    gather(r("osl"), r("y0g"), og)
-
-    def holder(i):
-        x = near[i] + sh
-        ts(r("oh", 6 * i, 6 * i + 6), r("n6"), r("bzf", x, x + 1), O.add)
-    holder(0)
-    holder(1)
-    tt(r("m32"), r("sw"), r("dm"), O.mult, r("osl", 12, 14))
+    lin(r("y0g", 14, 96, 16), r("ones", *six), 0.0, r("cn", 6, 7))
+    lin(r("y0g", 16 * me + 14, 16 * me + 15), r("ones", 0, 1), 0.0, 0.0)
+    og, ofs = r("zg", em, em + 1), r("osl", 2, 14)
+    gather(r("osl"), r("yc"), og)
+    c0 = (chip + sh) // 2 * 2
+    gather(r("oh", 0, 16 * (chip + sh + 3 - c0)), r("y1g"), r("zg", c0, chip + sh + 3))
+    tt(r("m32"), r("sw"), r("dm"), O.mult, r("osl", 0, 2))
     gather_a(r("st"), r("sw"), ofs)
-    tt(r("sm"), r("sw"), r("bm"), O.add, r("osl", 0, 8))
+    tt(r("sm"), r("sw"), r("bm"), O.add, r("osl", 2, 10))
     scan(r("sq"), r("rsq"), r("m32"), O.mult)
     s0, s1 = r("sq", 15, 16), r("sq", 31, 32, 1, 64)
 
-    pick("hs", 0, 2 * TH, "hp", 0, 192, r("oh"), [(0, 192)])
-    for x, y in zip(("hs", "hs_s"), both("w0", HX + TH * third(me), HX + TH * third(me) + TH)):
-        send([([z], all_eng[h_all * i:h_all * i + h_all], r(x, TH * i, TH * i + TH), y, "a3") for i, z in enumerate(near)],
-             r(x))
+    for i, x in enumerate(near):
+        pick("hs", TH * i, TH, "hp", 0, 192, r("oh", 16 * (x + sh - c0), 16 * (x + sh - c0) + 6), [(0, 192)])
+    for x, y in (("hs", "w0"), ("hs_s", "w0_s")):
+        send([([T.cores[z]], all_eng[h_all * i:h_all * i + h_all], r(x, TH * i, TH * i + TH),
+               r(y, slot(z, me), slot(z, me) + TH), "a3") for i, z in enumerate(near)], r(x))
 
     lin(r("sgn", 0, 192, 1, 64), lower("st"), -1.0, s1, F.Sign)
     gather_a(r("l16"), r("y0g"), og)
-    lin(r("ct", 1, 768, 4, 64), r("sgn", 0, 192, 1, 64), -1.0, 0.0, F.Relu)
-    gts = gt_ops("st", s0, s1)
-    low1("st")
-    tie0(s0)
-    gts[0]()
-    gts[1]()
-    tie1(s1)
-    ts(r("ofz"), ofs, float(HX - 1), O.min)
-    qz("cq", 0, 192, r("ct"))
+    lin(r("ct", 1, 768, 4, 64), r("sgn", 0, 192, 1, 64), -2.0, 0.0, F.Relu)
+    compare("st", s0, s1, False)
     mm(3, "oneq", 0, "cq", 0, 192)
 
-    pick("tz", 0, 192, "w0", 0, 576, r("ofz"), [(0, 576)])
-    note(1, 1.0 / 16)
+    pick("tz", 0, 192, "w0", 0, HX, ofs, [(0, HX)])
     for k in range(4):
         mm(4 + k, "eq", 128 * k, "tz", 0, 192)
-    for k in range(2):
-        ac(r("d%d" % k), r("ps%d" % (4 + k), 0, 192))
     select(r("sc"), r("ps3", 0, 192), 0, 192)
-    ts(r("tk", 0, 1), r("zg", em, em + 1), r("cn", 9, 10), O.not_equal, r("cn", 6, 7), O.mult)
     ts(r("roc"), r("sc", 15, 192, 16), corr, O.subtract, K - 1.0, O.min)
-    ts(r("fm", 0, 12), r("sc", 15, 192, 16), r("tk", 0, 1), O.is_lt)
-    for k in (2, 3):
-        gather_a(r("g%d" % k), r("dn", K * k, K * k + K), r("roc"))
-
-    def make(k):
-        if k < 2:
-            tt(r("vn", k, 768, 4), r("dn", K * k, K * k + K), r("d%d" % k), O.add, r("roc"))
-        else:
+    ts(r("fm", 0, 12), r("sc", 15, 192, 16), r("l16", 14, 15), O.is_lt)
+    for k in range(4):
+        if k % 2:
+            gather_a(r("g%d" % k), r("dn", K * k, K * k + K), r("roc"))
             tt(r("vn", k, 768, 4), r("ps%d" % (4 + k), 0, 192), r("g%d" % k), O.add)
-    make(0)
+        else:
+            ac(r("d%d" % k), r("ps%d" % (4 + k), 0, 192))
+            tt(r("vn", k, 768, 4), r("dn", K * k, K * k + K), r("d%d" % k), O.add, r("roc"))
     tt(r("fl", 0, 12), r("fm", 0, 12), r("cnx"), O.mult)
-    make(1)
-    tt(r("fl", 0, 12), r("fl", 0, 12), r("l16", 0, 12), O.max)
-    make(2)
-    make(3)
+    tt(r("fl", 0, 12), r("fl", 0, 12), r("l16", 2, 14), O.max)
     cp(r("ofin"), r("fl", 0, 12))
     qz("w0", NX, 192, r("vn"))
-    pick("fin", 0, 128, "w0", 0, 1152, r("ofin", 0, 8), [(0, 1152)])
-    pick("fin", 128, 64, "w0", 0, 1152, r("ofin", 8, 12), [(0, 1152)])
+    pick("fin", 0, 128, "w0", 0, NX + P, r("ofin", 0, 8), [(0, NX + P)])
+    pick("fin", 128, 64, "w0", 0, NX + P, r("ofin", 8, 12), [(0, NX + P)])
 
     mm(1, "wq", 0, "fin", 0, 128)
     mm(2, "wq", 128, "fin", 0, 128)
     mm(3, "wq", 128, "fin", 64, 128)
     mm(0, "wq", 0, "fin", 64, 128)
+    dma("s", T.od[:, :], r("odt", 0, 12, 1, 0, 1), "dout", 128)
     dma("s", T.oc[:, :], r("fin"), "dout", 128)
     for k in range(4):
-        dma("s" if k < 3 else "a", T.osc[4 * k:4 * k + 4, :], r("fin_s", 0, 192, 1, 32 * k, 32 * k + 4), "dout", 128)
+        dma("s" if k < 3 else "a", T.osc[4 * k:4 * k + 4, :], r("fin_s", 0, 192, 1, 32 * k, 32 * k + 4), "dout", 128, time=0.6)
     cp(r("ysb", 0, 128), r("ps1", 0, 128))
     ac(r("ysb", 192, 320), r("ps2", 0, 128))
-    ac(r("ysb", 320, 384), r("ps3", 64, 128))
+    cp(r("ysb", 320, 384), r("ps3", 64, 128))
     cp(r("ysb", 128, 192), r("ps0", 64, 128))
     dma("s", T.y[:, 0:192], r("ysb", 0, 192), "dout", 128)
     dma("a", T.y[:, 192:384], r("ysb", 192, 384), "dout", 128)
-    dma("s", T.od[:, :], r("odt", 0, 12, 1, 0, 1), "dout", 128)
 
+    for j in plan(ops):
+        calls[j]()
     for q in count:
         due["c" + q] = count[q]
-    for s in sorted(due):
+    for s in sorted(due, key=lambda s: s == "dout"):
         g.wait_ge(T.sem[s], due[s])

from concourse.bass import DstId, RemoteDMATransfer
from concourse.mybir import dt, AluOpType as O, ActivationFunctionType as F

P, K, N = 192, 48, 6
LX, PAD, HX, NX = 288, 576, 592, 976
TH = 96
BIG = 1e29
STEP = 2048.0

SCRATCH = {}
ARENA = {}
for _d, _l in (
        ("bfloat16", "ut 4 tbt 768 nzt 704 wt 1024 ubt 512 half 516 eht 516 vt 512 vn 768 ct 768 x48 288 pos 288 psc 288 "
                     "wct 512 irb 384"),
        ("int32", "pi 4 pa 6 hi 8 fb 16"),
        ("float32", "ipd 128 i16 32 ir 8 m16 4 t16 192 dq 192 ones 32 paf 6 pf 2 cn 24 bm 128 dm 32 nw 4 nws 4 nr8 8 "
                    "rsq 32 c48 8 sm 128 sm1 64 sg 192 sg1 192 sc 192 sc2 192 "
                    "msgf 2 sw 592 dn 192 d0 192 g1 192 d2 192 g3 192 v1r 16 rke 16 cnx 12 n16 96 y1g 96 bzf 8 sgn 192 "
                    "st 192 m32 32 sq 32 ysb 384 odt 16 rho 136 tm 64 t1 64 t2 128 dl 8 hq 16 ca 96 hb 96 hc 96 sb 96 sd 96 "
                    "rg 96"),
        ("uint16", "land 48 odl 8 l6 6 ol 12 oll 4 om 4 ox 4 ob 6 zg 16 osl 16 oh 64 roc 12 ofin 12 pt 8")):
    _w = _l.split()
    for _k, _n in zip(_w[::2], _w[1::2]):
        SCRATCH[_k] = ("sbuf", [128, int(_n)], _d)
_w = "tq 192 nq 176 wq 256 uq 128 oneq 256 eq 512 cq 192 nb 192 hp 192 hr 96 hs 192 lb 128 tz 192 w0 1168 fin 192".split()
for _k, _n in zip(_w[::2], _w[1::2]):
    SCRATCH[_k] = ("sbuf", [128, int(_n)], "float8_e4m3fn_x4")
    SCRATCH[_k + "_s"] = ("sbuf", [128, int(_n)], "uint8")
for _k in range(8):
    SCRATCH["ps%d" % _k] = ("psum", [128, 512], "float32")
_o = 0
for _n, _l in ((96, "y0g yt yc"),
               (16, "key ks zr0 zr1 wr0 wr1 wf wc cz fa l16 fl fm"),
               (8, "gt pl t5 t0 k2 nc8 ap3 fan r96 r144 u1 v1 c1 bz cb hb2 hc2 tk vf h2 hf")):
    for _k in _l.split():
        ARENA[_k] = (_o, _n)
        _o += _n + (-_n) % 8
SCRATCH["ar"] = ("sbuf", [128, _o], "float32")

DMAS = ["du", "dtb", "dnz", "dw", "dpv", "dpad", "dhb", "dout", "dct", "dvn"]
SEMAPHORES = ["cv", "ca", "ct", "cg", "am", "al", "ah", "ax", "an", "a3", "left", "r0", "r1"] + DMAS


def r(name, a=0, b=None, step=1, p=0, q=128):
    o, n = ARENA[name] if name in ARENA else (0, SCRATCH[name][1][1])
    return ("ar" if name in ARENA else name, p, q, o + a, o + (n if b is None else b), step)


def meet(x, y):
    return (x[0] == y[0] and x[1] < y[2] and y[1] < x[2] and x[3] < y[4] and y[3] < x[4]
            and not (x[5] == y[5] and (x[3] - y[3]) % x[5]))


def covers(x, y):
    return x[1] <= y[1] and y[2] <= x[2] and x[3] <= y[3] and y[4] <= x[4] and (x[5] == 1 or x[5] == y[5] and x[3] == y[3])


WAKE = 0.16
ORDER = [int(_k) for _k in """
33 0 52 50 10 11 12 13 15 14 34 16 17 1 2 3 4 5 6 7 8 9 36 37 49 39 51 78 54 42 38 47 43 40 46 44 58 48 45 53 79 81 80 82 83 84
88 87 91 93 90 92 89 94 71 76 85 86 68 55 60 95 96 97 101 98 102 103 113 114 104 99 100 105 75 106 115 107 121 77 108 57 56 59
122 63 62 67 61 134 116 109 111 24 25 19 26 110 112 119 117 120 73 123 74 118 72 135 136 148 137 138 139 150 149 151 124 130 140
158 157 132 133 131 125 127 18 21 23 27 30 31 32 22 28 20 35 126 128 141 142 143 144 152 145 70 147 191 165 192 195 171 69 129
155 154 166 156 153 208 230 207 197 198 169 167 170 168 159 172 175 160 176 174 161 173 146 188 189 186 187 190 177 41 178 162
163 200 196 209 201 199 193 211 203 194 202 216 210 204 212 205 179 65 64 164 231 233 232 218 234 221 220 214 213 215 222 66 180
183 29 181 182 184 185 217 224 219 235 239 228 229 236 223 238 225 240 206 242 244 243 226 237 241 245 247 246 249 248 227
250 254 255 256 258 259 252 257 268 270 279 261 263 253 269 251 307 271 272 273 274 275 260 276 278 262 277 280 282 281 283 264
266 265 267 284 286 285 295 287 291 289 293 288 296 292 290 294 297 298 299 301 300 302 312 303 306 304 305 309 311 310 308 313
316 315 314 318 317
""".split() if _k.isdigit()]
PLAN = {}


def plan(ops):
    n = len(ops)
    pre = [dict() for _ in range(n)]
    seen = {}
    for j, (q, rs, ws, _, _, after) in enumerate(ops):
        for i in after:
            pre[j][i] = 0.0
        for x, w in [(x, False) for x in rs] + [(x, True) for x in ws]:
            bank = SCRATCH[x[0]][0] == "psum"
            for i, y, v in seen.get(x[0], ()):
                if i != j and not q == "x" == ops[i][0] and ((w or v) and meet(x, y) or bank and ops[i][0] != q):
                    pre[j][i] = 0.0 if q == "t" == ops[i][0] else WAKE
        for x, w in [(x, False) for x in rs] + [(x, True) for x in ws]:
            seen.setdefault(x[0], []).append((j, x, w))
    PLAN["ops"], PLAN["pre"] = ops, pre
    where = {j: k for k, j in enumerate(ORDER)}
    if len(where) == n and all(where[i] < where[j] for j in range(n) for i in pre[j]):
        return ORDER
    PLAN["bad"] = True
    return list(range(n))


def rank_program(g, core, T, topo):
    def far_of(x):
        return [y for y in range(N) if topo.chip(T.cores[y]) != topo.chip(T.cores[x])]

    def near_of(x):
        return [y for y in range(N) if y != x and y not in far_of(x)]

    def third(x):
        return [y for y in range(N) if y not in far_of(x)].index(x)

    def mate_of(x):
        return [y for y in far_of(x) if third(y) == third(x)][0]

    def helper(x):
        c = T.cores[x]
        here = [y for y in [x] + near_of(x) if topo.die(T.cores[y]) == topo.die(c)]
        if 2 * len(here) <= len(near_of(x)) + 1:
            return None
        free = [d for d in topo.cores_of(c) if topo.die(d) != topo.die(c) and T.rank_of(d) is None
                and topo.may_write(d, T.cores[mate_of(x)])]
        return free[sorted(here).index(x)]

    def address(c):
        a = topo.addr(c)
        return DstId(rid=a[0], pnc=a[1])

    me = T.rank_of(core)
    if me is None:
        for x in range(N):
            if helper(x) == core:
                to = T.cores[mate_of(x)]
                n_in = len(topo.engines(T.cores[x], core)) - len(topo.engines(T.cores[x], to))
                for sem, a, b in (("r0", T["hr"][:, 0:TH].bitcast(dt.uint8), T["hp"][:, TH:2 * TH].bitcast(dt.uint8)),
                                  ("r1", T["hr_s"][:, 0:TH], T["hp_s"][:, TH:2 * TH])):
                    g.wait_ge(T.sem[sem], n_in)
                    g.remote_dma_fused([RemoteDMATransfer(dst_ids=[address(to)], dma_engine_mask=topo.mask(core, to),
                                                          remote_sem=T.sem["ah"], srcs=[a], dsts=[b])], local_sem=T.sem["left"])
                g.wait_ge(T.sem["left"], 2 * len(topo.engines(core, to)))
        return
    queue = {"v": g.vector, "a": g.scalar, "t": g.tensor, "g": g, "s": g.sync}
    V, A, X = g.vector, g.scalar, g.tensor
    count = {"v": 0, "a": 0, "t": 0, "g": 0}
    clk = {q: {} for q in queue}
    snap, wr, rd, due = {}, {}, {}, {}

    def wait(q, s, v):
        if clk[q].get(s, 0) < v:
            queue[q].wait_ge(T.sem[s], v)
            for s2, v2 in snap.get((s, v), {}).items():
                clk[q][s2] = max(clk[q].get(s2, 0), v2)
            clk[q][s] = v

    def before(q, reads, writes, adds=False):
        need = {}
        for x in reads + writes:
            bank = SCRATCH[x[0]][0] == "psum"
            hits = [(y, tok) for y, tok in wr.get(x[0], ()) if meet(x, y) or bank and tok[0] != "c" + q]
            if x in writes:
                hits += [(y, tok) for y, tok in rd.get(x[0], ()) if meet(x, y) or bank and tok[0] != "c" + q]
            elif bank:
                hits += [(y, tok) for y, tok in rd.get(x[0], ()) if tok[0] != "c" + q]
            for y, tok in hits:
                if bank and adds and tok[0] == "c" + q:
                    continue
                need[tok[0]] = max(need.get(tok[0], 0), tok[1])
        for s in sorted(need):
            wait(q, s, need[s])

    def wrote(x, tok):
        for d in (wr, rd):
            d[x[0]] = [e for e in d.get(x[0], ()) if not covers(x, e[0])]
        wr[x[0]].append((x, tok))

    ops, calls = [], []

    def width(x):
        return (x[4] - x[3] + x[5] - 1) // x[5]

    def narrow(*xs):
        return 0.5 if all(SCRATCH[x[0]][2] in ("bfloat16", "uint16") for x in xs) else 1.0

    def issue(q, reads, writes, fn, sem=None, total=0, adds=False, time=None, per=1.0):
        if time is None:
            time = {"v": 0.04, "a": 0.08}[q] + max(0.053, 0.00083 * per * width(writes[0]))
        ops.append((q, reads, writes, 0.05 if sem else time, time, []))
        calls.append(lambda: emit(q, reads, writes, fn, sem, total, adds))

    def emit(q, reads, writes, fn, sem, total, adds):
        before(q, reads, writes, adds)
        if sem is None:
            count[q] += 1
            tok = ("c" + q, count[q])
            fn().then_inc(T.sem[tok[0]], 1)
            snap[tok] = dict(clk[q])
        else:
            tok = (sem, total)
            fn().then_inc(T.sem[sem], 16)
            due[sem] = total
        for x in reads:
            rd.setdefault(x[0], []).append((x, tok))
        for x in writes:
            wrote(x, tok)

    def ap(x, bits=None):
        v = T[x[0]][x[1]:x[2], x[3]:x[4]:x[5]] if x[5] > 1 else T[x[0]][x[1]:x[2], x[3]:x[4]]
        return v.bitcast(bits or dt.uint8) if SCRATCH[x[0]][2] == "float8_e4m3fn_x4" else v

    def mx(x):
        return T[x[0]][:, x[3]:x[4]]

    def num(s):
        return ap(s) if isinstance(s, tuple) else s

    def ts(out, in0, s1, op0, s2=None, op1=None):
        rs = [in0] + [s for s in (s1, s2) if isinstance(s, tuple)]
        if op1 is None:
            issue("v", rs, [out], lambda: V.tensor_scalar(ap(out), ap(in0), num(s1), None, op0), per=narrow(out, in0))
        else:
            issue("v", rs, [out], lambda: V.tensor_scalar(ap(out), ap(in0), num(s1), num(s2), op0, op1), per=narrow(out, in0))

    def tt(out, a, b, op, off=None):
        if off is None:
            issue("v", [a, b], [out], lambda: V.tensor_tensor(ap(out), ap(a), ap(b), op),
                  per=1 if "psum" in (SCRATCH[a[0]][0], SCRATCH[b[0]][0]) else 2)
        else:
            issue("v", [a, b, off], [out], lambda: V.tensor_tensor(ap(out), ap(a).indirect(ap(off)), ap(b), op),
                  time=0.05 + 0.0013 * width(out))

    def cp(out, in_):
        issue("v", [in_], [out], lambda: V.tensor_copy(ap(out), ap(in_)))

    def turn(out, in_):
        issue("v", [in_], [out], lambda: V.transpose(ap(out), ap(in_)))

    def ac(out, in_):
        issue("a", [in_], [out], lambda: A.activation(ap(out), ap(in_), F.Copy))

    def lin(out, in_, scale, bias, func=F.Identity):
        rs = [in_] + ([bias] if isinstance(bias, tuple) else [])
        issue("a", rs, [out], lambda: A.activation(ap(out), ap(in_), func, bias=num(bias), scale=scale))

    def gather(out, win, off):
        issue("v", [win, off], [out], lambda: V.tensor_copy(ap(out), ap(win).indirect(ap(off))),
              time=0.05 + 0.0013 * width(out))

    def gather_a(out, win, off, scale=1.0):
        issue("a", [win, off], [out], lambda: A.activation(ap(out), ap(win).indirect(ap(off)), F.Identity, scale=scale),
              time=0.065 + 0.0013 * width(out))

    def scatter(win, val, off):
        issue("v", [val, off], [win], lambda: V.tensor_copy(ap(win).indirect(ap(off)), ap(val)), time=0.1)

    def scan(out, keep, add, op0=O.min, op1=O.add):
        issue("v", [keep, add], [out], lambda: V.tensor_tensor_scan(ap(out), ap(keep), ap(add), 0.0, op0, op1),
              per=narrow(out, keep, add))

    corr = r("cn", 0, 1)

    def select(out, val, a, b):
        scan(out, r("dq", a, b), val, O.add, O.max)

    def fill(x, c):
        issue("v", [], [x], lambda: V.memset(ap(x), c), per=narrow(x))

    def both(name, a, b):
        return [r(name, a, b), r(name + "_s", a, b)]

    def qz(cod, o, n, tile):
        c, s = both(cod, o, o + n)
        issue("v", [tile], [c, s], lambda: V.quantize_mx(mx(c), mx(s), ap(tile)), time=0.012 + 0.00088 * n)

    def mm(k, lhs, lo, rhs, ro, n, start=True, stop=True):
        w, x, out = both(lhs, lo, lo + 128), both(rhs, ro, ro + n), r("ps%d" % k, 0, n)
        issue("t", w + x, [out], lambda: X.matmul_mx(ap(out), mx(w[0]), mx(w[1]), mx(x[0]), mx(x[1]), start, stop),
              adds=not start, time=0.00116 * (n + 16))

    def pick(dst, c, n, src, a, b, off, parts):
        do, so, wc, ws = r(dst, c, c + n), r(dst + "_s", c, c + n), r(src, a, b), r(src + "_s", a, b)
        issue("v", [r(src, x, y) for x, y in parts] + [off], [do], lambda: V.tensor_copy(
            ap(do, dt.uint32), ap(wc, dt.uint32).indirect(ap(off))), time=0.05 + 0.0013 * n)
        issue("a", [r(src + "_s", x, y) for x, y in parts] + [off], [so], lambda: A.activation(
            ap(so), ap(ws).indirect(ap(off)), F.Copy), time=0.065 + 0.0013 * n)

    def iota(x, pattern, base, cm):
        if SCRATCH[x[0]][2] == "int32":
            issue("g", [], [x], lambda: g.iota(ap(x), pattern, base, cm), time=0.13 + 0.00166 * width(x))
        else:
            issue("g", [], [x], lambda: g.iota(ap(x), pattern, base, cm, allow_small_or_imprecise_dtypes=True),
                  time=0.13 + 0.00166 * width(x))

    def choose(out, in_, pattern, op, other, base, cm):
        issue("g", [in_], [out], lambda: g.affine_select(ap(out), ap(in_), pattern, op, other, base, cm),
              time=0.17 + 0.00166 * width(out))

    def dma(q, out, in_, sem, total=16, behind=(), time=0.8):
        issue(q, ([in_] if isinstance(in_, tuple) else []) + list(behind), [out] if isinstance(out, tuple) else [],
              lambda: queue[q].dma_start(num(out), num(in_)), sem, total, time=time)

    def move(dst, a, src, b, n, sem, total=32, behind=()):
        for x, y in zip(both(dst, a, a + n), both(src, b, b + n)):
            dma("s", x, y, sem, total, behind)

    sh = me % 2
    e6, em = (sh, sh + 6), me + sh
    others = [x for x in range(N) if x != me]

    def slot(x, y):
        return HX + TH * (2 + near_of(x).index(y))
    far, near, mate = far_of(me), near_of(me), mate_of(me)
    all_eng = topo.engines(core, T.cores[near[0]])
    out_eng = topo.engines(core, T.cores[far[0]])
    in_eng = [e for e in all_eng if e not in out_eng]

    def mask(es):
        return sum(1 << e for e in es)

    lands, sent = {}, []

    def send(transfers, src, behind=()):
        ops.append(("g", [src] + list(behind), [], 0.25, 0.25, sent[-1:]))
        calls.append(lambda: remote(transfers, [src] + list(behind)))
        sent.append(len(ops) - 1)
        for sem in sorted(set(e[4] for e in transfers), key=lambda s: s == "an"):
            ops.append(("x", [], lands[sem], 0.0, 1.3 if len(sent) > 1 else 2.4, sent[-1:]))
            calls.append(lambda: None)

    def remote(transfers, reads):
        before("g", reads, [])
        due["left"] = due.get("left", 0) + sum(len(e[1]) for e in transfers)
        g.remote_dma_fused([RemoteDMATransfer(dst_ids=[address(y) for y in x], dma_engine_mask=mask(es), remote_sem=T.sem[sem],
                                              srcs=[ap(s)], dsts=[ap(to)] * len(x)) for x, es, s, to, sem in transfers],
                           local_sem=T.sem["left"])

    def spread(src, sem, sem2=None):
        send([([T.cores[x] for x in far], out_eng, src, src, sem), ([T.cores[x] for x in near], in_eng, src, src, sem2 or sem)],
             src)

    def to_mate(k):
        src = both("hp", 0, TH)[k]
        if helper(me) is None:
            send([([T.cores[mate]], out_eng, src, both("hp", TH, 2 * TH)[k], "ah")], src)
        else:
            send([([helper(me)], in_eng, src, both("hr", 0, TH)[k], "r%d" % k)], src)

    h_all = len(all_eng) // 2
    n_all = sum(len(out_eng) if x in far else len(in_eng) for x in others)
    for sem, tot, whom, buf, base, w in (("al", 2 * n_all, others, "w0", lambda x: K * x, K),
                                         ("ax", 2 * len(out_eng) * len(far), far, "w0", lambda x: LX + K * x, K),
                                         ("an", 2 * len(in_eng) * len(near), near, "w0", lambda x: LX + K * x, K),
                                         ("ah", 2 * len(out_eng), [mate], "hp", lambda x: TH, TH),
                                         ("a3", 2 * h_all * len(near), near, "w0", lambda x: slot(me, x), TH)):
        due[sem] = tot
        for x in whom:
            for e in both(buf, base(x), base(x) + w):
                wrote(e, (sem, tot))
                lands.setdefault(sem, []).append(e)
    due["am"] = n_all
    lands["r0"] = lands["r1"] = lands["ah"]
    for x in others:
        wrote(r("land", 8 * x, 8 * x + 1), ("am", n_all))
        lands.setdefault("am", []).append(r("land", 8 * x, 8 * x + 1))

    dma("a", r("ut"), T.u[:, 0:4], "du", time=0.6)
    dma("s", r("tbt"), T.tb[:, :], "dtb")
    for buf in ("ct", "vn"):
        dma("s", r(buf, 0, 384), T.u[:, 128:512], "d" + buf, 32, [r("tbt")] if buf == "vn" else [], time=1.3)
        dma("s", r(buf, 384, 768), T.u[:, 128:512], "d" + buf, 32, time=1.3)
    dma("s", r("nzt", 0, 384), T.nz[:, :], "dnz", 32, time=2.0)
    dma("s", r("nzt", 384, 704), T.nz[:, 0:320], "dnz", 32, time=2.0)
    dma("s", r("vt", 192, 512), T.tb[:, 0:320], "dpv", time=2.0)
    dma("s", r("wt"), T.w[:, :], "dw", time=2.6)

    six = (0, 6)
    iota(r("pi"), [[16 - sh, 2], [0, 2]], 0, 1)
    iota(r("pf"), [[64, 2]], 0, 1)
    iota(r("ipd"), [[1, 128]], 0, -1)
    iota(r("t16"), [[0, 12], [1, 16]], 0, 0)
    iota(r("t16", 0, 192, 16), [[0, 12]], -1000, 0)
    iota(r("irb"), [[1, 192], [0, 2]], 0, 0)
    iota(r("ir"), [[1, 8]], 0, 0)
    iota(r("m16"), [[16, 4]], 0, 0)
    iota(r("dl"), [[16, 2], [32, 2], [0, 2]], 0, 0)
    iota(r("rke"), [[1, 16]], -sh, 0)
    iota(r("n16"), [[0, 6], [16, 16]], 0, 0)
    iota(r("c48"), [[48, 8]], 0, 0)
    iota(r("cnx"), [[16, 12]], NX, 0)
    iota(r("hq"), [[0, 16]], 0, 0)
    iota(r("fb"), [[0, 16]], 0, 0)
    iota(r("key"), [[0, 16]], -100, 0)
    iota(r("tm"), [[0, 64]], 0, 0)
    iota(r("ones"), [[0, 32]], 1, 0)
    iota(r("i16"), [[0, 2], [1, 16]], 0, 0)
    iota(r("x48"), [[0, 6], [1000, 48]], 0, 0)
    for x in [me] + near:
        a, b = (HX, HX + TH) if x == me else (slot(me, x),) * 2
        if mate_of(x) < x:
            a, b = b, a
        lo, step = min(x, mate_of(x)) + sh, abs(x - mate_of(x))
        iota(r("hq", lo, lo + step + 1, step), [[b - a, 2]], a - 2 * K, 0)

    fill(r("half"), 0.5)
    choose(r("eht"), r("half"), [[1, 516]], O.is_equal, 0.0, -3, -4)
    choose(r("rsq"), r("ones"), [[0, 2], [1, 16]], O.not_equal, 0.0, 0, 0)
    ts(r("pa", 0, 4), r("pi"), 15, O.bitwise_and)
    ts(r("pa", 4, 6), r("pi", 0, 2), 1, O.bitwise_and)
    qz("oneq", 0, 128, r("half", 0, 512))
    cp(r("paf"), r("pa"))
    own = r("paf", 0, 1)
    lin(r("bm"), r("ipd"), -3e29, 1.5e29, F.Relu)
    ts(r("dm"), r("i16"), own, O.is_equal)
    ts(r("cn", 2, 3), r("paf", 2, 3), -3.0, O.add, 2.5, O.max)
    for k in range(2):
        lin(r("cn", 16 + k, 17 + k), own, -1.0, r("pf", k, k + 1))
        lin(r("wct", k, 512, 4), r("half", 0, 128), 0.0, own)
        lin(r("wct", 2 + k, 512, 4), r("half", 0, 128), 0.0, r("cn", 16 + k, 17 + k))
    for k in range(4):
        if k % 2:
            lin(r("ubt", k, 512, 4), r("half", 0, 128), 0.0, r("ut", k, k + 1))
        else:
            ts(r("ubt", k, 512, 4), r("half", 0, 128), r("ut", k, k + 1), O.mult, 2.0, O.mult)
    lin(r("cn", 1, 2), own, -STEP, -STEP / 2)
    qz("uq", 0, 128, r("ubt"))
    lin(corr, own, 32.0, -480.0, F.Square)
    lin(r("nr8", *six), r("ir", *six), -0.125, 0.0)
    lin(r("nc8", *six), r("ir", *six), -0.125, corr)
    lin(r("cn", 5, 6), own, 32.0, -32.0 * (sh + 5), F.Square)
    lin(r("nw", 0, 3), r("m16", 0, 3), 1.0, own)
    lin(r("cn", 3, 4), r("cn", 5, 6), 1.0, corr)
    lin(r("nws", 0, 3), r("nw", 0, 3), 1.0 / K, 0.0)
    lin(r("cn", 9, 10), r("paf", 4, 5), 61.0, 2.0)
    lin(r("cn", 6, 7), corr, 1.0, float(K))
    lin(r("v1r"), r("rke"), 16.0, own)
    lin(r("n16"), r("n16"), 1.0, own)
    lin(r("cnx"), r("cnx"), 1.0, own)
    lin(r("cn", 4, 5), own, 3.0, r("cn", 9, 10))
    lin(r("dq"), r("t16"), STEP, r("cn", 1, 2))
    cp(r("l6"), r("ir", *six))
    ts(r("odl"), r("dl"), own, O.add)
    qz("oneq", 128, 128, r("wct"))
    for k in range(4):
        qz("eq", 128 * k, 128, r("eht", 3 - k, 515 - k))
    qz("nq", 0, 176, r("nzt"))
    qz("wq", 0, 256, r("wt"))

    qz("tq", 0, 192, r("tbt"))
    mm(0, "uq", 0, "tq", 0, 192)
    mm(1, "tq", 0, "uq", 0, 128)
    mm(2, "tq", 64, "uq", 0, 128)
    mm(6, "uq", 0, "tq", 0, 192)
    move("lb", K, "tq", K, 80, "dpad", 32)

    lin(r("sg"), r("ps6", 0, 192), 1.0, 0.0, F.Sign)
    issue("a", [r("sg")], [r("sg1"), r("msgf", 0, 1)], lambda: A.activation(
        ap(r("sg1")), ap(r("sg")), F.Relu, accum_out=ap(r("msgf", 0, 1))))

    def lower(src, a=0, b=192):
        return r(src, a, b, 1, 64, 128)

    def compare(src, sp0, sp1, all_):
        tt(r("sm1", 0, 64, 1, 64), lower(src, 128), r("bm", 64, 128, 1, 64), O.add)
        ts(r("ct", 0, 512, 4), r(src, 0, 128), sp0, O.is_gt, 2.0, O.mult)
        ts(r("ct", 512, 768, 4), r(src, 128, 192), sp0, O.is_ge, 2.0, O.mult)
        if all_:
            ts(r("ct", 1, 768, 4, 64), lower(src), sp1, O.is_gt, 2.0, O.mult)
        ts(r("ct", 2, 512, 4), r("sm"), sp0, O.is_equal, 2.0, O.mult)
        ts(r("ct", 515, 768, 4, 64), r("sm1", 0, 64, 1, 64), sp1, O.is_equal, 2.0, O.mult)
        qz("cq", 0, 192, r("ct"))

    def listed(out, a, b, src):
        select(r("sc2", a, b), src, a, b)
        ts(out, r("sc2", a + 15, b, 16), corr, O.subtract)

    tt(r("sm"), r("ps0", 0, 128), r("bm"), O.add)
    compare("ps0", r("ps1", 0, 1), r("ps2", 0, 1, 1, 64), True)
    mm(4, "cq", 0, "oneq", 0, 128)
    mm(5, "cq", 64, "oneq", 0, 128)

    def order(k, a, b, n):
        ts(r("vn", 4 * a, 4 * b, 2), r("irb", 2 * a, 2 * b), r("ps4", 0, 1), O.is_equal)
        ts(r("vn", 4 * a + 1, 4 * b, 2, 64), r("irb", 2 * a, 2 * b, 1, 64), r("ps5", 0, 1, 1, 64), O.is_equal)
        qz("cq", a, n, r("vn", 4 * a, 4 * a + 4 * n))
        mm(k, "oneq", 128, "cq", a, n)

    my_land = r("land", 8 * me, 8 * me + 1)
    ts(r("land", 8 * me, 8 * me + 1, 1, 0, 64), r("msgf", 0, 1, 1, 0, 64), 256.0, O.mult, r("ps4", 0, 1, 1, 0, 64), O.add)
    ts(r("land", 8 * me, 8 * me + 1, 1, 64), r("ps5", 0, 1, 1, 64), 256.0, O.mult, r("ps4", 0, 1, 1, 64), O.add)
    spread(my_land, "am")
    order(3, 0, K, 128)
    listed(r("ol", 0, 3), 0, 48, r("ps3", 0, 48))
    pick("w0", K * me, K, "tq", 0, 192, r("ol", 0, 3), [(0, 192)])
    for x in both("w0", K * me, K * me + K):
        spread(x, "al")
    order(2, K, P, P - K)
    listed(r("om", 0, 3), 48, 96, r("ps2", 0, 48))
    listed(r("ol", 6, 12), 96, 192, r("ps2", 48, 144))
    pick("w0", PAD, HX - PAD, "tq", 0, 192, r("ol", 0, 1), [(0, 192)])
    pick("hp", 0, TH, "tq", 0, 192, r("ol", 6, 12), [(0, 192)])
    to_mate(0)
    to_mate(1)
    pick("nb", 0, 48, "tq", 0, 192, r("om", 0, 3), [(0, 192)])

    def noise(t, stop):
        for k in range(4):
            mm(4 + k, "eq", 128 * k, "nq", K * t, 128, True, stop)
    noise(0, False)

    def places(k, ref, val, zr):
        pu, tpu = r("pt", 4 * k, 4 * k + 1), r("pt", 4 * k + 2, 4 * k + 3)
        pl, t5 = r("pl", k, k + 1), r("t5", k, k + 1)
        issue("a", [r("k2", *six), ref], [r("gt", *six), pl], lambda: A.activation(
            ap(r("gt", *six)), ap(r("k2", *six)), F.Sign, bias=ap(ref), scale=-1.0, accum_out=ap(pl)), time=0.155)
        ts(pu, pl, -0.5, O.mult, r("cn", 2, 3), O.add)
        ts(t5, pl, -1.0, O.mult, pl, O.max)
        scatter(r("wr%d" % k), val, pu)
        ts(tpu, t5, -0.5, O.mult, 2.5, O.add)
        gather(zr, r("wr%d" % k), tpu)
        lin(r("odt", 6 * k, 6 * k + 6), r("wr%d" % k, *six), 1.0 / 16 if k else 1.0, 0.0)
        return pu, tpu

    for k in (0, 64):
        ts(r("fb", sh, sh + 6, 1, k, k + 64), r("land", 0, 48, 8, 0, 64), 1.0 / 256, O.mult, -127.5 / 256, O.add)
    tt(r("key", *e6), r("fb", *e6), r("nr8", *six), O.add)
    tt(r("k2", *six), r("fb", *e6), r("nc8", *six), O.add)
    select(r("ks"), r("key"), 0, 16)
    pu, tpu = places(0, r("ks", 15, 16), r("rke"), r("zr0"))
    ts(r("oll", 0, 3), r("nws", 0, 3), r("zr0", em, em + 1), O.add, float(K), O.mult)

    ts(r("hi", *six), r("land", 0, 48, 8), 1.0 / 256, O.mult, -127.5 / 256, O.add)
    cp(r("vf", *six), r("land", 0, 48, 8))
    cp(r("hf", *six), r("hi", *six))
    ts(r("h2", *six), r("hf", *six), -256.0, O.mult)
    tt(r("rho", 2, 8), r("h2", *six), r("vf", *six), O.add)
    for k in range(6):
        src = r("rho", 2, 8, 1, 32 * k, 32 * k + 32) if k < 4 else r("hf", 0, 6, 1, 32 * k - 64, 32 * k - 32)
        ac(r("tm", 6 * k, 6 * k + 6, 1, 0, 32), src)
    for k in (32, 64):
        cp(r("tm", 0, 36, 1, k, 2 * k), r("tm", 0, 36, 1, 0, k))
    turn(r("t1"), r("tm"))
    gather(r("t2"), r("t1"), r("odl"))
    turn(r("rho", 8, 136), r("t2"))
    ac(r("rho", 66, 72), r("hf", *six))

    pick("lb", 0, 48, "w0", 0, 288, r("oll", 0, 3), [(0, 288)])
    for k in range(4):
        mm(4 + k, "eq", 128 * k, "lb", 0, 128, False, True)
    ts(r("tk", 0, 1), r("zr0", em, em + 1), float(me), O.not_equal, 64.0, O.mult)
    ts(r("ox", 0, 3), r("nw", 0, 3), r("tk", 0, 1), O.add)
    for k in range(4):
        (cp if k else ac)(r("vt", k, 192, 4), r("ps%d" % (4 + k), 0, 48))
    qz("nb", 64, 128, r("vt"))
    pick("w0", LX + K * me, K, "nb", 0, 192, r("ox", 0, 3), [(0, 48), (64, 192)])
    for x in both("w0", LX + K * me, LX + K * me + K)[::-1]:
        spread(x, "ax", "an")
    noise(1, True)
    mm(1, "uq", 0, "w0", 0, 288)

    scatter(r("wf"), r("fb"), pu)
    gather(r("fa"), r("wf"), tpu)
    scatter(r("wc"), r("hq"), pu)
    gather(r("cz"), r("wc"), tpu)
    tt(r("t0", *six), r("zr0", *e6), r("ir", *six), O.not_equal)
    ts(r("ob"), r("zr0", *e6), r("cn", 4, 5), O.add)
    lin(r("r96", *six), r("fa", *e6), 1.0, float(K - P + K), F.Relu)
    lin(r("r144", *six), r("fa", *e6), 1.0, float(K - P), F.Relu)
    tt(r("fan", *six), r("fa", *e6), r("nr8", *six), O.add)
    tt(r("u1", *six), r("r96", *six), r("r144", *six), O.subtract)
    tt(r("v1", *six), r("u1", *six), r("r144", *six), O.subtract)
    tt(r("fan", *six), r("fan", *six), r("u1", *six), O.subtract)
    tt(r("v1", *six), r("v1", *six), r("t0", *six), O.mult)
    tt(r("key", *e6), r("fan", *six), r("v1", *six), O.add)
    select(r("ks"), r("key"), 0, 16)
    ts(r("ap3", *six), r("key", *e6), r("ks", 15, 16), O.subtract, r("cn", 3, 4), O.add)
    lin(r("c1", *six), r("t0", *six), float(LX), 0.0)
    lin(r("bz", *six), r("zr0", *e6), float(K), float(LX - K))
    tt(r("c1", *six), r("c1", *six), r("c48", *six), O.add)
    tt(r("hc2", *six), r("cz", *e6), r("bz", *six), O.subtract)
    tt(r("hb2", *six), r("bz", *six), r("c1", *six), O.subtract)
    tt(r("cb", *six), r("cz", *e6), r("c1", *six), O.add)
    gather_a(r("hc"), r("hc2"), r("l6"), 0.5)
    gather_a(r("hb"), r("hb2"), r("l6"), 0.5)
    gather_a(r("ca"), r("cb"), r("l6"), 0.5)
    ts(r("bzf", *six), r("zr0", *e6), *((min(far) - 0.5, O.is_gt) if me < min(far) else (max(far) + 0.5, O.is_lt)), TH, O.mult)
    tt(r("y1g"), r("bzf"), r("n16"), O.add, r("l6"))
    gather_a(r("rg"), r("rho"), r("ob"))
    tt(r("yt"), r("rho"), r("ca"), O.add, r("ob"))
    lin(r("sb"), r("rg"), 1.0, 0.5 - K, F.Sign)
    lin(r("sd"), r("rg"), 1.0, 0.5 - 2 * K, F.Sign)
    ac(r("sw", 0, 288), r("ps1", 0, 288))
    tt(r("sb"), r("sb"), r("hb"), O.mult)
    tt(r("sd"), r("sd"), r("hc"), O.mult)
    tt(r("yt"), r("yt"), r("sb"), O.add)
    tt(r("y0g"), r("yt"), r("sd"), O.add)
    ts(r("yc"), r("y0g"), float(PAD), O.min)
    move("w0", HX, "hp", 0, 2 * TH, "dhb", 32, both("w0", LX + K * min(far), LX + K * max(far) + K))
    lin(r("sw", PAD, HX), r("ones", 0, 16), 0.0, BIG)
    for k in range(4):
        ac(r("dn", K * k, K * k + K), r("ps%d" % (4 + k), 0, K))

    chip = min([me] + near)
    for k, a in ((0, K * chip), (2, K * min(far))):
        mm(k, "uq", 0, "w0", LX + a, 144)
        ts(r("pos", a, a + 144), r("ps%d" % k, 0, 144), 0.0, O.is_gt)
        ac(r("sw", LX + a, LX + a + 144), r("ps%d" % k, 0, 144))
        scan(r("psc", a, a + 144), r("x48", a, a + 144), r("pos", a, a + 144))
    scan(r("ks", *six), r("dq", *e6), r("psc", 47, 288, 48), O.add, O.max)
    tt(r("k2", *six), r("psc", 47, 288, 48), r("ap3", *six), O.add)
    pu, tpu = places(1, r("ks", 5, 6), r("v1r"), r("zg"))
    lin(r("y0g", 14, 96, 16), r("ones", *six), 0.0, r("cn", 6, 7))
    lin(r("y0g", 16 * me + 14, 16 * me + 15), r("ones", 0, 1), 0.0, 0.0)
    og, ofs = r("zg", em, em + 1), r("osl", 2, 14)
    gather(r("osl"), r("yc"), og)
    c0 = (chip + sh) // 2 * 2
    gather(r("oh", 0, 16 * (chip + sh + 3 - c0)), r("y1g"), r("zg", c0, chip + sh + 3))
    tt(r("m32"), r("sw"), r("dm"), O.mult, r("osl", 0, 2))
    gather_a(r("st"), r("sw"), ofs)
    tt(r("sm"), r("sw"), r("bm"), O.add, r("osl", 2, 10))
    scan(r("sq"), r("rsq"), r("m32"), O.mult)
    s0, s1 = r("sq", 15, 16), r("sq", 31, 32, 1, 64)

    for i, x in enumerate(near):
        pick("hs", TH * i, TH, "hp", 0, 192, r("oh", 16 * (x + sh - c0), 16 * (x + sh - c0) + 6), [(0, 192)])
    for x, y in (("hs", "w0"), ("hs_s", "w0_s")):
        send([([T.cores[z]], all_eng[h_all * i:h_all * i + h_all], r(x, TH * i, TH * i + TH),
               r(y, slot(z, me), slot(z, me) + TH), "a3") for i, z in enumerate(near)], r(x))

    lin(r("sgn", 0, 192, 1, 64), lower("st"), -1.0, s1, F.Sign)
    gather_a(r("l16"), r("y0g"), og)
    lin(r("ct", 1, 768, 4, 64), r("sgn", 0, 192, 1, 64), -2.0, 0.0, F.Relu)
    compare("st", s0, s1, False)
    mm(3, "oneq", 0, "cq", 0, 192)

    pick("tz", 0, 192, "w0", 0, HX, ofs, [(0, HX)])
    for k in range(4):
        mm(4 + k, "eq", 128 * k, "tz", 0, 192)
    select(r("sc"), r("ps3", 0, 192), 0, 192)
    ts(r("roc"), r("sc", 15, 192, 16), corr, O.subtract, K - 1.0, O.min)
    ts(r("fm", 0, 12), r("sc", 15, 192, 16), r("l16", 14, 15), O.is_lt)
    for k in range(4):
        if k % 2:
            gather_a(r("g%d" % k), r("dn", K * k, K * k + K), r("roc"))
            tt(r("vn", k, 768, 4), r("ps%d" % (4 + k), 0, 192), r("g%d" % k), O.add)
        else:
            ac(r("d%d" % k), r("ps%d" % (4 + k), 0, 192))
            tt(r("vn", k, 768, 4), r("dn", K * k, K * k + K), r("d%d" % k), O.add, r("roc"))
    tt(r("fl", 0, 12), r("fm", 0, 12), r("cnx"), O.mult)
    tt(r("fl", 0, 12), r("fl", 0, 12), r("l16", 2, 14), O.max)
    cp(r("ofin"), r("fl", 0, 12))
    qz("w0", NX, 192, r("vn"))
    pick("fin", 0, 128, "w0", 0, NX + P, r("ofin", 0, 8), [(0, NX + P)])
    pick("fin", 128, 64, "w0", 0, NX + P, r("ofin", 8, 12), [(0, NX + P)])

    mm(1, "wq", 0, "fin", 0, 128)
    mm(2, "wq", 128, "fin", 0, 128)
    mm(3, "wq", 128, "fin", 64, 128)
    mm(0, "wq", 0, "fin", 64, 128)
    dma("s", T.od[:, :], r("odt", 0, 12, 1, 0, 1), "dout", 128)
    dma("s", T.oc[:, :], r("fin"), "dout", 128)
    for k in range(4):
        dma("s" if k < 3 else "a", T.osc[4 * k:4 * k + 4, :], r("fin_s", 0, 192, 1, 32 * k, 32 * k + 4), "dout", 128, time=0.6)
    cp(r("ysb", 0, 128), r("ps1", 0, 128))
    ac(r("ysb", 192, 320), r("ps2", 0, 128))
    cp(r("ysb", 320, 384), r("ps3", 64, 128))
    cp(r("ysb", 128, 192), r("ps0", 64, 128))
    dma("s", T.y[:, 0:192], r("ysb", 0, 192), "dout", 128)
    dma("a", T.y[:, 192:384], r("ysb", 192, 384), "dout", 128)

    for j in plan(ops):
        calls[j]()
    for q in count:
        due["c" + q] = count[q]
    for s in sorted(due, key=lambda s: s == "dout"):
        g.wait_ge(T.sem[s], due[s])
